import numpy as np, ml_dtypes
CORES = [13,21,141,149]
N = 4
import mx_ref
BF = ml_dtypes.bfloat16
def cols(t, e):
    v = np.concatenate([t.reshape(128, -1, 4), np.zeros((128, 1, 4), BF)], axis=1)
    return np.ascontiguousarray(v[:, e]).reshape(128, -1)
def cut(t, i, w=512):
    return t[:, w * i:w * i + w]
def f(rng, *shape):
    return mx_ref.flush((rng.standard_normal(shape, dtype=np.float32) * np.exp2(rng.integers(-2, 3, shape[:-1] + (1,)))).astype(BF))
def wide(rng, *shape, cols=0):
    v = rng.standard_normal(shape, dtype=np.float32) * np.exp2(rng.integers(-12, 13, shape)).astype(np.float32)
    if cols: v *= np.repeat(np.exp2(rng.integers(-cols, cols + 1, shape[:-2] + (1, shape[-1] // 4))) * (rng.random(shape[:-2] + (1, shape[-1] // 4)) > 0.0625), 4, axis=-1).astype(np.float32)
    return mx_ref.flush(v.astype(BF))
T, CAPP = 512, 48
def normal(rng, *shape):
    return mx_ref.flush(rng.standard_normal(shape, dtype=np.float32).astype(BF))
def once(rng, case):
    g = wide if case == "spread" else normal
    c = g(rng, N, 128, 4 * T).transpose(1, 0, 2).reshape(128, N * T, 4)
    v = (wide if case == "spread" else f)(rng, N, 128, 4 * T)
    if case in ("near", "ties"):
        e = np.stack([q * T + rng.permutation(T) for q in range(N)])
        m = T // 16; s = int(rng.integers(1, N))
        sets = [(e[:, :2 * m], np.roll(e[:, 2 * m:4 * m], -s, axis=0)),
                (e[:, 4 * m:7 * m], e[:, 7 * m:10 * m]),
                (e[:, 10 * m:11 * m], e[:, 11 * m:12 * m], e[:, 12 * m:13 * m]),
                (e[:, 13 * m:14 * m], e[:, 14 * m:15 * m], np.roll(e[:, 15 * m:], -s, axis=0))]
        first, at, place = np.zeros(N * T, int), np.zeros(N * T, int), rng.integers(0, 512, N * T)
        for l in sets:
            l = np.sort(np.stack(l), axis=0)
            for i in range(len(l)):
                first[l[i]] = l[0]; at[l[i]] = i; place[l[i]] = place[l[0]]
        c = c[:, first]
        if case == "near": c[place // 4, np.arange(N * T), place % 4] = (1 + 0.25 * at).astype(BF)
    if case == "negative":
        z = normal(rng, 128, 1, 4).astype(np.float32) * np.float32(2.0 ** 20)
        c = mx_ref.flush((c.astype(np.float32) * np.float32(2.0 ** 20) + z).astype(BF))
    an, fb = [], []
    for r in range(N):
        if case == "ties":
            n = rng.permutation([CAPP, CAPP, 128 - 2 * CAPP, 0]); to = []
            for q in range(N):
                w = rng.choice(q * T + np.flatnonzero(at[q * T:q * T + T] < 2), n[q])
                w[:12] = w[:1]; to += list(w)
            to = np.array(to)
        else:
            n = 24 + rng.multinomial(32, np.full(N, np.divide(1, N)))
            while n.max() > 40: n = 24 + rng.multinomial(32, np.full(N, np.divide(1, N)))
            to = np.repeat(np.arange(N) * T, n) + rng.integers(0, T, 128)
        to = rng.permutation(to)
        other = (to + rng.integers(1, N * T, 128)) % (N * T)
        away = (to + rng.integers(1, N * T, 128)) % (N * T)
        h = rng.permutation(128) < (128 if case == "forbid" else 64 if case in ("plain", "spread") else 0)
        best, second = np.where(h, other, to), np.where(h, to, other)
        ban = np.where(h, other, away)
        if case == "ties": ban = np.where(at[to] > 0, first[to], away)
        t = c[:, best].astype(np.float32) + np.float32(0.5) * c[:, second].astype(np.float32)
        if case == "negative": t = t - np.float32(4.5) * z
        if case == "near":
            t[place[to] // 4, np.arange(128), place[to] % 4] = np.where(at[to] > 0, 1, -1) * np.exp2(-rng.integers(1, 6, 128))
        an.append(mx_ref.flush(t.astype(BF)).reshape(128, 512)); fb.append(ban.astype(np.int32).reshape(128, 1))
    k = np.ascontiguousarray(c.reshape(128, N, 4 * T).transpose(1, 0, 2))
    return {"an": np.stack(an), "k": k, "v": v, "u": f(rng, N, 128, 512), "fb": np.stack(fb)}
def planted(d, case):
    if case not in ("near", "negative", "ties"): return True
    s = scores(d["an"], d["k"])
    if case == "negative": return bool((s < 0).all())
    s = allowed(s, d["fb"])
    if case == "near":
        top = np.partition(s, N * T - 2, axis=1)[:, -2:]
        gap = top[:, 1] - top[:, 0]
        return bool(((gap > 0) & (gap < 2.0 ** -9 * np.abs(top[:, 1]))).sum(axis=1).min() >= 20)
    w = np.argmax(s, axis=1)
    per = (s == s.max(axis=1, keepdims=True)).reshape(N, N, T, 128).sum(axis=2)
    within = np.take_along_axis(per, (w // T)[:, None], axis=1)[:, 0] > 1
    across = (per > 0).sum(axis=1) > 1
    return bool(within.sum(axis=1).min() >= 10 and across.sum() >= 20)
def draw(rng, case):
    for _ in range(50):
        d = once(rng, case)
        if not check_inputs(d) and planted(d, case): return d
    raise RuntimeError("no draw in 50 tries: " + case)
def setup_inputs(rng):
    return draw(rng, "plain")
def setup_inputs_forbid(rng):
    return draw(rng, "forbid")
def setup_inputs_near(rng):
    return draw(rng, "near")
def setup_inputs_negative(rng):
    return draw(rng, "negative")
def setup_inputs_spread(rng):
    return draw(rng, "spread")
def setup_inputs_ties(rng):
    return draw(rng, "ties")
def scores(an, k):
    kq = [mx_ref.quantize(cut(k[q], j)) for q in range(N) for j in range(T // 128)]
    out = []
    for r in range(N):
        a = mx_ref.quantize(an[r])
        out.append(np.concatenate([mx_ref.matmul(b, a) for b in kq]))
    return np.stack(out)
def allowed(s, fb):
    for r in range(N): s[r][fb[r][:, 0], np.arange(128)] = -np.inf
    return s
def winners(an, k, fb):
    return np.argmax(allowed(scores(an, k), fb), axis=1)
def check_inputs(d):
    if d["fb"].min() < 0 or d["fb"].max() >= N * T: return ["fb"]
    b = []; w = winners(d["an"], d["k"], d["fb"])
    for r in range(N):
        if np.bincount(w[r] // T, minlength=N).max() > CAPP: b.append("winners")
    return b
def reference(an, k, v, u, fb):
    w = winners(an, k, fb)
    allv = np.concatenate([v[q] for q in range(N)], axis=1)
    y = np.zeros((N, 128, 128), np.float32)
    for r in range(N):
        y[r] = mx_ref.matmul(mx_ref.quantize(u[r]), mx_ref.quantize(cols(allv, w[r])))
    return {"y": y, "win": w.astype(np.float32).reshape(N, 128, 1)}

@@ -1,0 +1,406 @@
+from concourse.bass import DstId, RemoteDMATransfer
+from concourse.mybir import dt, AluOpType, AxisListType, ActivationFunctionType
+
+OP = AluOpType
+ACT = ActivationFunctionType
+C8 = "float8_e4m3fn_x4"
+FAR = 1.0e29
+
+SCRATCH = {
+    "at": ("sbuf", [128, 512], "bfloat16"),
+    "kt": ("sbuf", [128, 2048], "bfloat16"),
+    "vt": ("sbuf", [128, 2048], "bfloat16"),
+    "ut": ("sbuf", [128, 512], "bfloat16"),
+    "fbd": ("dram", [128, 1], "int32"),
+    "fbo": ("sbuf", [128, 1], "int32"),
+    "qa": ("sbuf", [128, 128], C8), "qas": ("sbuf", [128, 128], "uint8"),
+    "qk": ("sbuf", [128, 512], C8), "qks": ("sbuf", [128, 512], "uint8"),
+    "qu": ("sbuf", [128, 128], C8), "qus": ("sbuf", [128, 128], "uint8"),
+    "la": ("sbuf", [128, 512], C8), "las": ("sbuf", [128, 512], "uint8"),
+    "lf": ("sbuf", [128, 4], "int32"),
+    "best": ("sbuf", [128, 16], "float32"),
+    "lz": ("sbuf", [128, 512], C8), "lzs": ("sbuf", [128, 512], "uint8"),
+    "lc": ("sbuf", [128, 4], "float32"), "ln": ("sbuf", [128, 4], "float32"),
+    "rfb": ("dram", [128, 1], "int32"),
+    "rac": ("sbuf", [128, 128], C8), "ras": ("sbuf", [128, 128], "uint8"),
+    "rbest": ("sbuf", [128, 2], "float32"),
+    "rzc": ("sbuf", [128, 128], C8), "rzs": ("sbuf", [128, 128], "uint8"),
+    "ones": ("sbuf", [128, 512], "float32"),
+    "num": ("sbuf", [128, 512], "float32"),
+    "im": ("sbuf", [128, 64], "int32"), "am": ("sbuf", [128, 64], "int32"),
+    "mask": ("sbuf", [128, 64], "float32"),
+    "keep": ("sbuf", [128, 128], "float32"),
+    "ip": ("sbuf", [128, 4], "int32"), "i1": ("sbuf", [128, 4], "int32"),
+    "i2": ("sbuf", [128, 4], "int32"), "i3": ("sbuf", [128, 4], "int32"),
+    "cp": ("sbuf", [128, 4], "float32"), "cd": ("sbuf", [128, 4], "float32"),
+    "cq": ("sbuf", [128, 4], "float32"), "nq": ("sbuf", [128, 4], "float32"),
+    "mx": ("sbuf", [128, 1], "float32"), "t4": ("sbuf", [128, 4], "float32"),
+    "c1": ("sbuf", [128, 4], "float32"), "c2": ("sbuf", [128, 4], "float32"),
+    "c3": ("sbuf", [128, 4], "float32"),
+    "pick": ("sbuf", [128, 1], "float32"), "won": ("sbuf", [128, 1], "float32"),
+    "xf": ("sbuf", [128, 64], "float32"), "yf": ("sbuf", [128, 64], "float32"),
+    "wf": ("sbuf", [128, 64], "float32"), "of": ("sbuf", [128, 8], "uint16"),
+    "prod": ("sbuf", [128, 512], "float32"),
+    "ysb": ("sbuf", [128, 128], "float32"),
+    "ps": ("psum", [128, 2048], "float32"),
+    "pu": ("psum", [128, 2048], "float32"),
+}
+for _i in range(4):
+    SCRATCH["fn%d" % _i] = ("sbuf", [128, 1], "float32")
+    SCRATCH["pen%d" % _i] = ("sbuf", [128, 512], "float32")
+    SCRATCH["ms%d" % _i] = ("sbuf", [128, 512], "float32")
+    SCRATCH["run%d" % _i] = ("sbuf", [128, 520], "float32")
+    SCRATCH["sink%d" % _i] = ("sbuf", [128, 512], "bfloat16")
+for _j in range(2):
+    SCRATCH["ab%d" % (_j + 2)] = ("sbuf", [128, 512], "bfloat16")
+    SCRATCH["x%d" % _j] = ("sbuf", [128, 128], "float32")
+    SCRATCH["xt%d" % _j] = ("sbuf", [128, 128], "float32")
+    SCRATCH["xw%d" % _j] = ("sbuf", [128, 128], "float32")
+    SCRATCH["off%d" % _j] = ("sbuf", [128, 16], "uint16")
+    SCRATCH["z%d" % _j] = ("sbuf", [128, 1024], "bfloat16")
+    SCRATCH["zq%d" % _j] = ("sbuf", [128, 256], C8)
+    SCRATCH["zqs%d" % _j] = ("sbuf", [128, 256], "uint8")
+
+SEMAPHORES = (
+    ["ld_a", "ld_k", "ld_v", "ld_u", "ld_fd", "ld_fo", "st"]
+    + ["sf", "sx", "sp", "sb", "sz"]
+    + ["rf_in", "rac_in", "ras_in", "rb_in", "rzc_in", "rzs_in", "rsent", "lc_in", "ln_in"]
+    + ["%s%d" % (n, i) for n in ("a_in", "f_in", "b_in", "z_in") for i in range(4)]
+    + ["k0", "k1", "k2", "k3", "k4", "k5", "qa_ok", "qk_ok", "qu_ok", "ab_ok2", "ab_ok3", "half2"]
+    + ["%s%d" % (n, i) for n in ("fn_ok", "pen_ok", "mm_ok", "ms_ok", "run_ok", "idx_ok", "pu_ok") for i in range(4)]
+    + ["%s%d" % (n, j) for n in ("x_ok", "xt_ok", "xw_ok", "o1_ok", "o2_ok", "zv_ok", "zs_ok", "zq_ok") for j in range(2)]
+    + ["m1", "m2", "m3", "m4", "m5", "pick_ok", "won_ok", "xf_ok", "yf_ok", "wf_ok", "of1_ok", "of2_ok", "uv", "us", "y_ok"]
+)
+
+
+def bits(engines):
+    m = 0
+    for e in engines:
+        m |= 1 << e
+    return m
+
+
+def roads(T, topo):
+    relay = {}
+    for r, a in enumerate(T.cores):
+        for d, b in enumerate(T.cores):
+            if d == r or topo.may_write(a, b):
+                continue
+            near = topo.host(a) == topo.host(b)
+            c = [x for x in topo.cores_of(a) if x != a and topo.may_write(x, b) and (topo.die(x) == topo.die(a)) == near]
+            relay[(r, d)] = c[0]
+    return relay
+
+
+def u8(view):
+    return view.bitcast(dt.uint8)
+
+
+def rank_program(g, core, T, topo):
+    relay = roads(T, topo)
+    rank = T.rank_of(core)
+    if rank is None:
+        for (r, d), c in relay.items():
+            if c == core:
+                relay_program(g, core, T, topo, r, d, min(q for q, b in relay if b == d) == r)
+        return
+    S = T.sem
+    V, P, A, Y = g.vector, g.tensor, g.scalar, g.sync
+    direct = [d for d in range(len(T.cores)) if d != rank and (rank, d) not in relay]
+    cross = [d for d in range(len(T.cores)) if (rank, d) in relay]
+    cross.sort(key=lambda d: topo.die(relay[(rank, d)]) != topo.die(core))
+    mate = direct[0]
+    order = [rank, mate] + cross
+    n = {}
+
+    def done(q, name, k=1):
+        q.then_inc(S[name], k)
+        n[name] = n.get(name, 0) + k
+
+    def need(queue, *names):
+        for x in names:
+            queue.wait_ge(S[x], n[x])
+
+    done(Y.dma_start(T.at[:], T.an[:]), "ld_a", 16)
+    done(A.dma_start(T.fbd[:], T.fb[:]), "ld_fd", 16)
+    done(A.dma_start(T.fbo[:], T.fb[:]), "ld_fo", 16)
+    done(Y.dma_start(T.kt[:], T.k[:]), "ld_k", 16)
+
+    done(g.iota(T.im[:], [[-16, 2], [0, 2], [-1, 16]], 64, 1), "k0")
+    done(V.memset(T.ones[:], 1.0), "k1")
+    done(V.memset(T.keep[:], 1.0), "k1")
+    need(V, "k1")
+    done(V.tensor_tensor_scan(T.num[:], T.ones[:], T.ones[:], -1.0, OP.add, OP.mult), "k2")
+    done(V.memset(T.keep[:, 0:128:32], 0.0), "k2")
+    need(V, "ld_a")
+    done(V.quantize_mx(T.qa[:], T.qas[:], T.at[:]), "qa_ok")
+    need(V, "k0")
+    done(V.tensor_scalar(T.am[:], T.im[:], 31, None, OP.bitwise_and), "k3")
+    need(V, "k3")
+    done(V.tensor_scalar(T.mask[:], T.am[:], 0.0, 4.0, OP.is_equal, OP.mult), "k4")
+
+    far = topo.engines(core, T.cores[mate])
+    chip = topo.engines(core, relay[(rank, cross[0])])
+    rest = [e for e in chip if e not in far]
+
+    def xfer(dst, mask, sem, src, to):
+        rid, pid = topo.addr(dst, core)
+        return RemoteDMATransfer(dst_ids=[DstId(rid=rid, pnc=pid)], dma_engine_mask=mask, remote_sem=S[sem], src=src, dst=to)
+
+    def fused(sem, *ts):
+        g.remote_dma_fused(list(ts), local_sem=S[sem])
+
+    rl = [relay[(rank, d)] for d in cross]
+    dm = T.cores[mate]
+    half = [bits(chip[1::2]), bits(chip[0::2])]
+    need(g, "ld_fd")
+    fused("sf",
+          xfer(rl[0], bits(rest[0:2]), "rf_in", T.fbd[:], T.rfb[:]),
+          xfer(rl[1], bits(rest[2:4]), "rf_in", T.fbd[:], T.rfb[:]),
+          xfer(dm, bits(far[0::2]), "f_in%d" % rank, T.fbd[:], T.lf[:, rank:rank + 1]))
+    n["sf"] = 2 + 2 + len(far[0::2])
+    need(g, "qa_ok")
+    fused("sx",
+          xfer(rl[0], half[0], "rac_in", u8(T.qa[:]), u8(T.rac[:])),
+          xfer(rl[1], half[1], "rac_in", u8(T.qa[:]), u8(T.rac[:])))
+    fused("sx",
+          xfer(rl[0], half[0], "ras_in", T.qas[:], T.ras[:]),
+          xfer(rl[1], half[1], "ras_in", T.qas[:], T.ras[:]))
+    n["sx"] = 2 * len(chip)
+    rid, pid = topo.addr(dm, core)
+    s = slice(128 * rank, 128 * rank + 128)
+    g.remote_dma(u8(T.la[:, s]), u8(T.qa[:]), S["a_in%d" % rank], S.sp, pid, rid, bits(far))
+    g.remote_dma(T.las[:, s], T.qas[:], S["a_in%d" % rank], S.sp, pid, rid, bits(far))
+    n["sp"] = 2 * len(far)
+
+    need(Y, "sx")
+    done(Y.dma_start(T.vt[:], T.v[:]), "ld_v", 16)
+    done(Y.dma_start(T.ut[:], T.u[:]), "ld_u", 16)
+
+    for i in (1, 2, 3):
+        q = order[i]
+        last = T.cores[q] if (q, rank) not in relay else relay[(q, rank)]
+        e = len(topo.engines(last, core))
+        n["a_in%d" % q] = 2 * e
+        n["z_in%d" % q] = 2 * e
+        n["b_in%d" % q] = e
+        n["f_in%d" % q] = e if i > 1 else len(topo.engines(last, core)[0::2])
+        if i > 1:
+            n["lc_in"] = n["ln_in"] = e
+
+    def forbidden(i):
+        q = order[i]
+        if i == 0:
+            need(V, "ld_fo")
+            src = T.fbo[:]
+        else:
+            need(V, "f_in%d" % q)
+            src = T.lf[:, q:q + 1]
+        done(V.tensor_scalar(T["fn%d" % i][:], src, float(512 * rank), None, OP.subtract), "fn_ok%d" % i)
+
+    def pen_v(i):
+        need(V, "fn_ok%d" % i, "k2")
+        done(V.tensor_scalar(T["pen%d" % i][:], T.num[:], T["fn%d" % i][:], FAR, OP.is_equal, OP.mult), "pen_ok%d" % i)
+
+    def pen_a(i):
+        need(A, "fn_ok%d" % i, "k2")
+        done(A.activation(T["ab%d" % i][:], T.num[:], ACT.Abs, bias=T["fn%d" % i][:], scale=-1.0), "ab_ok%d" % i)
+        need(A, "ab_ok%d" % i)
+        done(A.activation(T["pen%d" % i][:], T["ab%d" % i][:], ACT.Relu, bias=FAR, scale=-FAR), "pen_ok%d" % i)
+
+    def anchors(i):
+        q = order[i]
+        if i == 0:
+            need(P, "qa_ok", "qk_ok")
+            return T.qa[:], T.qas[:]
+        need(P, "a_in%d" % q)
+        return T.la[:, 128 * q:128 * q + 128], T.las[:, 128 * q:128 * q + 128]
+
+    def score(i):
+        l, ls = anchors(i)
+        done(P.matmul_mx(T.ps[:, 512 * i:512 * i + 512], l, ls, T.qk[:], T.qks[:], True, True), "mm_ok%d" % i)
+
+    def halves(i):
+        l, ls = anchors(i)
+        done(P.matmul_mx(T.ps[:, 512 * i:512 * i + 256], l, ls, T.qk[:, 0:256], T.qks[:, 0:256], True, True), "mm_ok%d" % i)
+        done(P.matmul_mx(T.pu[:, 512 * i:512 * i + 256], l, ls, T.qk[:, 256:512], T.qks[:, 256:512], True, True), "half%d" % i)
+
+    def top(i):
+        m, r, p = T["ms%d" % i], T["run%d" % i], T["pen%d" % i]
+        need(V, "pen_ok%d" % i, "mm_ok%d" % i)
+        if i == 2:
+            done(V.tensor_tensor(m[:, 0:256], T.ps[:, 512 * i:512 * i + 256], p[:, 0:256], OP.subtract), "ms_ok%d" % i)
+            need(V, "half%d" % i)
+            done(V.tensor_tensor(m[:, 256:512], T.pu[:, 512 * i:512 * i + 256], p[:, 256:512], OP.subtract), "ms_ok%d" % i)
+        else:
+            done(V.tensor_tensor(m[:], T.ps[:, 512 * i:512 * i + 512], p[:], OP.subtract), "ms_ok%d" % i)
+        need(V, "ms_ok%d" % i)
+        done(V.tensor_tensor_scan(r[:, 0:512], m[:], m[:], -FAR, OP.max, OP.max), "run_ok%d" % i)
+        need(A, "run_ok%d" % i)
+        done(A.activation(T["sink%d" % i][:], r[:, 0:512], ACT.Sign, bias=r[:, 511:512], scale=-1.0,
+                          accum_out=r[:, 512:513]), "idx_ok%d" % i)
+
+    forbidden(0)
+    pen_v(0)
+    need(V, "ld_k")
+    done(V.quantize_mx(T.qk[:], T.qks[:], T.kt[:]), "qk_ok")
+    score(0)
+    top(0)
+    forbidden(1)
+    pen_v(1)
+    forbidden(2)
+    forbidden(3)
+    pen_a(2)
+    pen_a(3)
+    score(1)
+    top(1)
+    halves(2)
+    score(3)
+    top(2)
+    top(3)
+
+    need(g, "idx_ok1", "idx_ok2", "idx_ok3")
+    slot = T.best[:, 4 * rank:4 * rank + 2]
+    fused("sb",
+          xfer(rl[0], bits(rest[1::2]), "rb_in", T.run2[:, 511:513], T.rbest[:]),
+          xfer(rl[1], bits(rest[0::2]), "rb_in", T.run3[:, 511:513], T.rbest[:]),
+          xfer(dm, bits(far), "b_in%d" % rank, T.run1[:, 511:513], slot))
+    n["sb"] = len(rest) + len(far)
+
+    def values(j, i0, i1):
+        x, xt, xw, o, z = T["x%d" % j], T["xt%d" % j], T["xw%d" % j], T["off%d" % j], T["z%d" % j]
+        for l, i in enumerate((i0, i1)):
+            need(V, "idx_ok%d" % i, "k4")
+            done(V.tensor_scalar(x[:, 64 * l:64 * l + 64], T.mask[:], T["run%d" % i][:, 512:513], None, OP.mult), "x_ok%d" % j)
+        need(V, "x_ok%d" % j)
+        done(V.transpose(xt[:], x[:]), "xt_ok%d" % j)
+        need(V, "xt_ok%d" % j)
+        done(V.tensor_tensor_scan(xw[:], T.keep[:], xt[:], 0.0, OP.mult, OP.add), "xw_ok%d" % j)
+        need(V, "xw_ok%d" % j)
+        for c in range(4):
+            b = 2 * (c % 2) + c // 2
+            for to in (c, c ^ 1):
+                done(V.tensor_copy(o[32 * to:32 * to + 32, b:16:4], xw[32 * c:32 * c + 32, 31:128:32]), "o1_ok%d" % j)
+        need(V, "o1_ok%d" % j)
+        done(V.tensor_copy(o[0:64, 1:16:2], o[64:128, 1:16:2]), "o2_ok%d" % j)
+        done(V.tensor_copy(o[64:128, 0:16:2], o[0:64, 0:16:2]), "o2_ok%d" % j)
+        need(V, "o2_ok%d" % j, "ld_v")
+        need(A, "o2_ok%d" % j, "ld_v")
+        for t in (0, 1):
+            done(V.tensor_copy(z[:, t:1024:4], T.vt[:, t:2048].indirect(o[:, 0:16])), "zv_ok%d" % j)
+        for t in (2, 3):
+            done(A.activation(z[:, t:1024:4], T.vt[:, t:2048].indirect(o[:, 0:16]), ACT.Copy), "zs_ok%d" % j)
+        need(V, "zv_ok%d" % j, "zs_ok%d" % j)
+        done(V.quantize_mx(T["zq%d" % j][:], T["zqs%d" % j][:], z[:]), "zq_ok%d" % j)
+
+    values(0, 2, 3)
+    need(g, "zq_ok0")
+    fused("sz",
+          xfer(rl[0], half[0], "rzc_in", u8(T.zq0[:, 0:128]), u8(T.rzc[:])),
+          xfer(rl[1], half[1], "rzc_in", u8(T.zq0[:, 128:256]), u8(T.rzc[:])))
+    fused("sz",
+          xfer(rl[0], half[0], "rzs_in", T.zqs0[:, 0:128], T.rzs[:]),
+          xfer(rl[1], half[1], "rzs_in", T.zqs0[:, 128:256], T.rzs[:]))
+    values(1, 1, 0)
+    need(g, "zq_ok1")
+    g.remote_dma(u8(T.lz[:, s]), u8(T.zq1[:, 0:128]), S["z_in%d" % rank], S.sz, pid, rid, bits(far))
+    g.remote_dma(T.lzs[:, s], T.zqs1[:, 0:128], S["z_in%d" % rank], S.sz, pid, rid, bits(far))
+    n["sz"] = 2 * len(chip) + 2 * len(far)
+
+    need(V, "ld_u")
+    done(V.quantize_mx(T.qu[:], T.qus[:], T.ut[:]), "qu_ok")
+    done(V.tensor_copy(slot, T.run0[:, 511:513]), "m1")
+    need(V, "m1", *["b_in%d" % q for q in order[1:]])
+    done(V.tensor_reduce(T.mx[:], T.best[:, 0:16:4], AxisListType.X, OP.max), "m2")
+    need(V, "m2")
+    done(V.tensor_scalar(T.t4[:], T.best[:, 0:16:4], T.mx[:], 4096.0, OP.is_lt, OP.mult), "m3")
+    need(V, "m3", "lc_in", "ln_in")
+    done(V.tensor_tensor(T.c1[:], T.t4[:], T.lc[:], OP.add), "m4")
+    done(V.tensor_tensor(T.c2[:], T.t4[:], T.ln[:], OP.add), "m4")
+    need(V, "m4")
+    done(V.tensor_reduce(T.pick[:], T.c1[:], AxisListType.X, OP.min), "pick_ok")
+    done(V.tensor_tensor(T.c3[:], T.c2[:], T.best[:, 1:16:4], OP.add), "m5")
+    need(V, "pick_ok", "m5")
+    done(V.tensor_scalar(T.xf[:], T.mask[:], T.pick[:], 0.25, OP.mult, OP.mult), "xf_ok")
+    done(V.tensor_reduce(T.won[:], T.c3[:], AxisListType.X, OP.min), "won_ok")
+    need(Y, "won_ok")
+    done(Y.dma_start(T.win[:], T.won[:]), "st", 16)
+    need(V, "xf_ok")
+    done(V.transpose(T.yf[:], T.xf[:]), "yf_ok")
+    need(V, "yf_ok")
+    done(V.tensor_tensor_scan(T.wf[:], T.keep[:, 0:64], T.yf[:], 0.0, OP.mult, OP.add), "wf_ok")
+    need(V, "wf_ok")
+    for c in range(4):
+        for to in (c, c ^ 1):
+            done(V.tensor_copy(T.of[32 * to:32 * to + 32, 2 * c:2 * c + 2], T.wf[32 * c:32 * c + 32, 31:64:32]), "of1_ok")
+    need(V, "of1_ok")
+    done(V.tensor_copy(T.of[0:64, 4:8], T.of[64:128, 4:8]), "of2_ok")
+    done(V.tensor_copy(T.of[64:128, 0:4], T.of[0:64, 0:4]), "of2_ok")
+
+    for i in range(4):
+        q = order[i]
+        if i == 0:
+            need(P, "qu_ok", "zq_ok1")
+            r, rs = T.zq1[:, 128:256], T.zqs1[:, 128:256]
+        else:
+            need(P, "z_in%d" % q)
+            r, rs = T.lz[:, 128 * q:128 * q + 128], T.lzs[:, 128 * q:128 * q + 128]
+        if i == 2:
+            need(P, "ms_ok2")
+        done(P.matmul_mx(T.pu[:, 512 * i:512 * i + 128], T.qu[:], T.qus[:], r, rs, True, True), "pu_ok%d" % i)
+        to, frm = T.prod[:, 128 * q:128 * q + 128], T.pu[:, 512 * i:512 * i + 128]
+        if i in (0, 2):
+            need(V, "pu_ok%d" % i)
+            done(V.tensor_copy(to, frm), "uv")
+        else:
+            need(A, "pu_ok%d" % i)
+            done(A.activation(to, frm, ACT.Copy), "us")
+    need(V, "of2_ok", "uv", "us")
+    done(V.tensor_copy(T.ysb[:], T.prod[:].indirect(T.of[:, 0:8])), "y_ok")
+    need(Y, "y_ok")
+    done(Y.dma_start(T.y[:], T.ysb[:]), "st", 16)
+    need(Y, "st")
+    need(g, "sf", "sp", "sb", "sz")
+
+
+def relay_program(g, core, T, topo, r, d, place):
+    S = T.sem
+    V = g.vector
+    dst = T.cores[d]
+    rid, pid = topo.addr(dst, core)
+    m = topo.mask(core, dst)
+    e = len(topo.engines(core, dst))
+    if place:
+        g.iota(T.ip[:], [[0, 4]], 0, 1).then_inc(S.k0, 1)
+        g.iota(T.cp[:], [[128, 4]], 0, 1, allow_small_or_imprecise_dtypes=True).then_inc(S.k0, 1)
+        V.wait_ge(S.k0, 2)
+        V.tensor_scalar(T.i1[:], T.ip[:], 4, 1, OP.arith_shift_right, OP.bitwise_and).then_inc(S.k3, 1)
+        V.tensor_scalar(T.i2[:], T.ip[:], 6, None, OP.arith_shift_right).then_inc(S.k3, 1)
+        V.wait_ge(S.k3, 2)
+        V.tensor_tensor(T.i3[:], T.i1[:], T.i2[:], OP.subtract).then_inc(S.k4, 1)
+        V.wait_ge(S.k4, 1)
+        V.tensor_scalar(T.cd[:], T.i3[:], 48.0, None, OP.mult).then_inc(S.k5, 1)
+        V.wait_ge(S.k5, 1)
+        V.tensor_tensor(T.cq[:], T.cp[:], T.cd[:], OP.add).then_inc(S.k1, 1)
+        g.wait_ge(S.k1, 1)
+        g.remote_dma(T.lc[:], T.cq[:], S.lc_in, S.rsent, pid, rid, m)
+    else:
+        g.iota(T.nq[:], [[512, 4]], 0, 0, allow_small_or_imprecise_dtypes=True).then_inc(S.k0, 1)
+        g.wait_ge(S.k0, 1)
+        g.remote_dma(T.ln[:], T.nq[:], S.ln_in, S.rsent, pid, rid, m)
+    src = T.cores[r]
+    chip = topo.engines(src, core)
+    rest = [x for x in chip if x not in topo.engines(src, [c for i, c in enumerate(T.cores) if i != r and topo.may_write(src, c)][0])]
+    s = slice(128 * r, 128 * r + 128)
+    hops = [
+        ("rf_in", 2, T.lf[:, r:r + 1], T.rfb[:], "f_in"),
+        ("rac_in", len(chip) // 2, u8(T.la[:, s]), u8(T.rac[:]), "a_in"),
+        ("ras_in", len(chip) // 2, T.las[:, s], T.ras[:], "a_in"),
+        ("rb_in", len(rest) // 2, T.best[:, 4 * r:4 * r + 2], T.rbest[:], "b_in"),
+        ("rzc_in", len(chip) // 2, u8(T.lz[:, s]), u8(T.rzc[:]), "z_in"),
+        ("rzs_in", len(chip) // 2, T.lzs[:, s], T.rzs[:], "z_in"),
+    ]
+    for sem, k, to, frm, there in hops:
+        g.wait_ge(S[sem], k)
+        g.remote_dma(to, frm, S["%s%d" % (there, r)], S.rsent, pid, rid, m)
+    g.wait_ge(S.rsent, (1 + len(hops)) * e)

@@ -5,6 +5,8 @@ OP = AluOpType
 ACT = ActivationFunctionType
 C8 = "float8_e4m3fn_x4"
 FAR = 1.0e29
+A_, B_, D_ = 0, 1, 2
+JOBS = ("codes", "scales", "codes2", "scales2", "helper")
 
 SCRATCH = {
     "at": ("sbuf", [128, 512], "bfloat16"),
@@ -12,64 +14,58 @@ SCRATCH = {
     "vt": ("sbuf", [128, 2048], "bfloat16"),
     "ut": ("sbuf", [128, 512], "bfloat16"),
     "fbd": ("dram", [128, 1], "int32"),
-    "fbo": ("sbuf", [128, 1], "int32"),
-    "qa": ("sbuf", [128, 128], C8), "qas": ("sbuf", [128, 128], "uint8"),
-    "qk": ("sbuf", [128, 512], C8), "qks": ("sbuf", [128, 512], "uint8"),
+    "qx": ("sbuf", [128, 640], C8), "qxs": ("sbuf", [128, 640], "uint8"),
     "qu": ("sbuf", [128, 128], C8), "qus": ("sbuf", [128, 128], "uint8"),
-    "la": ("sbuf", [128, 512], C8), "las": ("sbuf", [128, 512], "uint8"),
+    "qv": ("sbuf", [128, 512], C8), "qvs": ("sbuf", [128, 512], "uint8"),
+    "la": ("sbuf", [128, 384], C8), "las": ("sbuf", [128, 384], "uint8"),
     "lf": ("sbuf", [128, 4], "int32"),
     "best": ("sbuf", [128, 16], "float32"),
-    "lz": ("sbuf", [128, 512], C8), "lzs": ("sbuf", [128, 512], "uint8"),
-    "lc": ("sbuf", [128, 4], "float32"), "ln": ("sbuf", [128, 4], "float32"),
-    "rfb": ("dram", [128, 1], "int32"),
+    "lz": ("sbuf", [128, 384], C8), "lzs": ("sbuf", [128, 384], "uint8"),
+    "lp": ("sbuf", [128, 4], "uint16"), "ln": ("sbuf", [128, 4], "bfloat16"),
+    "lo": ("sbuf", [128, 8], "uint16"),
+    "rfb": ("dram", [128, 1], "int32"), "rfd": ("dram", [128, 1], "int32"),
     "rac": ("sbuf", [128, 128], C8), "ras": ("sbuf", [128, 128], "uint8"),
     "rbest": ("sbuf", [128, 2], "float32"),
     "rzc": ("sbuf", [128, 128], C8), "rzs": ("sbuf", [128, 128], "uint8"),
-    "ones": ("sbuf", [128, 512], "float32"),
-    "num": ("sbuf", [128, 512], "float32"),
+    "hx": ("sbuf", [128, 640], C8), "hxs": ("sbuf", [128, 640], "uint8"),
+    "ones": ("sbuf", [128, 256], "bfloat16"),
+    "num": ("sbuf", [128, 256], "bfloat16"),
     "im": ("sbuf", [128, 64], "int32"), "am": ("sbuf", [128, 64], "int32"),
     "mask": ("sbuf", [128, 64], "float32"),
-    "keep": ("sbuf", [128, 128], "float32"),
-    "ip": ("sbuf", [128, 4], "int32"), "i1": ("sbuf", [128, 4], "int32"),
-    "i2": ("sbuf", [128, 4], "int32"), "i3": ("sbuf", [128, 4], "int32"),
-    "cp": ("sbuf", [128, 4], "float32"), "cd": ("sbuf", [128, 4], "float32"),
-    "cq": ("sbuf", [128, 4], "float32"), "nq": ("sbuf", [128, 4], "float32"),
-    "mx": ("sbuf", [128, 1], "float32"), "t4": ("sbuf", [128, 4], "float32"),
-    "c1": ("sbuf", [128, 4], "float32"), "c2": ("sbuf", [128, 4], "float32"),
-    "c3": ("sbuf", [128, 4], "float32"),
-    "pick": ("sbuf", [128, 1], "float32"), "won": ("sbuf", [128, 1], "float32"),
-    "xf": ("sbuf", [128, 64], "float32"), "yf": ("sbuf", [128, 64], "float32"),
-    "wf": ("sbuf", [128, 64], "float32"), "of": ("sbuf", [128, 8], "uint16"),
-    "prod": ("sbuf", [128, 512], "float32"),
+    "keep": ("sbuf", [128, 64], "float32"),
+    "ci": ("sbuf", [128, 4], "int32"), "cp": ("sbuf", [128, 4], "uint16"), "cn": ("sbuf", [128, 4], "bfloat16"),
+    "fn": ("sbuf", [128, 8], "float32"),
+    "ab": ("sbuf", [128, 512], "bfloat16"),
+    "x": ("sbuf", [128, 192], "float32"), "xt": ("sbuf", [128, 192], "float32"),
+    "xw": ("sbuf", [128, 768], "float32"), "off": ("sbuf", [128, 24], "uint16"),
+    "pos": ("sbuf", [128, 4], "float32"),
+    "mx": ("sbuf", [128, 1], "float32"), "lt": ("sbuf", [128, 4], "float32"), "gl": ("sbuf", [128, 4], "float32"),
+    "pick": ("sbuf", [128, 4], "float32"), "won": ("sbuf", [128, 4], "float32"),
+    "prod": ("sbuf", [128, 896], "float32"),
     "ysb": ("sbuf", [128, 128], "float32"),
     "ps": ("psum", [128, 2048], "float32"),
     "pu": ("psum", [128, 2048], "float32"),
 }
-for _i in range(4):
-    SCRATCH["fn%d" % _i] = ("sbuf", [128, 1], "float32")
-    SCRATCH["pen%d" % _i] = ("sbuf", [128, 512], "float32")
+for _i in range(2):
+    SCRATCH["pen%d" % _i] = ("sbuf", [128, 512], "bfloat16")
     SCRATCH["ms%d" % _i] = ("sbuf", [128, 512], "float32")
     SCRATCH["run%d" % _i] = ("sbuf", [128, 520], "float32")
     SCRATCH["sink%d" % _i] = ("sbuf", [128, 512], "bfloat16")
-for _j in range(2):
-    SCRATCH["ab%d" % (_j + 2)] = ("sbuf", [128, 512], "bfloat16")
-    SCRATCH["x%d" % _j] = ("sbuf", [128, 128], "float32")
-    SCRATCH["xt%d" % _j] = ("sbuf", [128, 128], "float32")
-    SCRATCH["xw%d" % _j] = ("sbuf", [128, 128], "float32")
-    SCRATCH["off%d" % _j] = ("sbuf", [128, 16], "uint16")
-    SCRATCH["z%d" % _j] = ("sbuf", [128, 1024], "bfloat16")
-    SCRATCH["zq%d" % _j] = ("sbuf", [128, 256], C8)
-    SCRATCH["zqs%d" % _j] = ("sbuf", [128, 256], "uint8")
+for _i in range(3):
+    SCRATCH["z%d" % _i] = ("sbuf", [128, 512], "bfloat16")
+    SCRATCH["zq%d" % _i] = ("sbuf", [128, 128], C8)
+    SCRATCH["zqs%d" % _i] = ("sbuf", [128, 128], "uint8")
 
 SEMAPHORES = (
-    ["ld_a", "ld_k", "ld_v", "ld_u", "ld_fd", "ld_fo", "st"]
-    + ["sf", "sx", "sp", "sb", "sz"]
-    + ["rf_in", "rac_in", "ras_in", "rb_in", "rzc_in", "rzs_in", "rsent", "lc_in", "ln_in"]
-    + ["%s%d" % (n, i) for n in ("a_in", "f_in", "b_in", "z_in") for i in range(4)]
-    + ["k0", "k1", "k2", "k3", "k4", "k5", "qa_ok", "qk_ok", "qu_ok", "ab_ok2", "ab_ok3", "half2"]
-    + ["%s%d" % (n, i) for n in ("fn_ok", "pen_ok", "mm_ok", "ms_ok", "run_ok", "idx_ok", "pu_ok") for i in range(4)]
-    + ["%s%d" % (n, j) for n in ("x_ok", "xt_ok", "xw_ok", "o1_ok", "o2_ok", "zv_ok", "zs_ok", "zq_ok") for j in range(2)]
-    + ["m1", "m2", "m3", "m4", "m5", "pick_ok", "won_ok", "xf_ok", "yf_ok", "wf_ok", "of1_ok", "of2_ok", "uv", "us", "y_ok"]
+    ["ld_a", "ld_k0", "ld_k1", "ld_v", "ld_u", "ld_fd", "ld_f", "st"]
+    + ["sf", "sx", "sk", "sent"]
+    + ["rf_in", "rd_in", "ra_in", "rb_in", "rz_in", "hx_in0", "hx_in1", "pos_in", "ln_in", "own_in", "lo_in"]
+    + ["%s%d" % (n, i) for n in ("a_in", "f_in", "b_in", "z_in") for i in range(3)]
+    + ["k0", "k1", "k2", "k3", "k4", "qa_ok", "qk_ok0", "qk_ok1", "qu_ok", "qv_ok", "ab_ok", "fn_ok"]
+    + ["%s%d" % (n, i) for n in ("pen_ok", "mm_ok", "half", "ms_ok", "run_ok", "idx_ok") for i in range(2)]
+    + ["%s%d" % (n, i) for n in ("zv_ok", "zs_ok", "zq_ok", "x_ok", "xt_ok", "xw_ok", "off_ok") for i in range(3)]
+    + ["pu_ok%d" % i for i in range(4)]
+    + ["m0", "m1", "m2", "m3", "pick_ok", "won_ok", "uv", "us", "yv_ok", "ys_ok"]
 )
 
 
@@ -80,37 +76,26 @@ def bits(engines):
     return m
 
 
-def roads(T, topo):
-    relay = {}
-    for r, a in enumerate(T.cores):
-        for d, b in enumerate(T.cores):
-            if d == r or topo.may_write(a, b):
-                continue
-            near = topo.host(a) == topo.host(b)
-            c = [x for x in topo.cores_of(a) if x != a and topo.may_write(x, b) and (topo.die(x) == topo.die(a)) == near]
-            relay[(r, d)] = c[0]
-    return relay
-
-
 def u8(view):
     return view.bitcast(dt.uint8)
 
 
-def rank_program(g, core, T, topo):
-    relay = roads(T, topo)
-    rank = T.rank_of(core)
-    if rank is None:
-        for (r, d), c in relay.items():
-            if c == core:
-                relay_program(g, core, T, topo, r, d, min(q for q, b in relay if b == d) == r)
-        return
+def team(T, topo, r):
+    me = T.cores[r]
+    others = [q for q in range(len(T.cores)) if q != r]
+    cross = sorted([q for q in others if not topo.may_write(me, T.cores[q])], key=lambda q: topo.host(T.cores[q]) != topo.host(me))
+    direct = [q for q in others if q not in cross]
+    free = [c for c in topo.cores_of(me) if c != me]
+    ports = [c for c in free if topo.may_write(c, T.cores[cross[0]])]
+    near = [c for c in ports if topo.die(c) == topo.die(me)]
+    far = [c for c in ports if c not in near]
+    helper = [c for c in free if c not in ports and topo.die(c) == topo.die(me)][0]
+    return {"ranks": cross + direct, "codes": far[0], "scales": near[0], "codes2": far[1], "scales2": near[1], "helper": helper}
+
+
+def tools(g, core, T, topo):
     S = T.sem
-    V, P, A, Y = g.vector, g.tensor, g.scalar, g.sync
-    direct = [d for d in range(len(T.cores)) if d != rank and (rank, d) not in relay]
-    cross = [d for d in range(len(T.cores)) if (rank, d) in relay]
-    cross.sort(key=lambda d: topo.die(relay[(rank, d)]) != topo.die(core))
-    mate = direct[0]
-    order = [rank, mate] + cross
+    V, P, A = g.vector, g.tensor, g.scalar
     n = {}
 
     def done(q, name, k=1):
@@ -121,286 +106,280 @@ def rank_program(g, core, T, topo):
         for x in names:
             queue.wait_ge(S[x], n[x])
 
-    done(Y.dma_start(T.at[:], T.an[:]), "ld_a", 16)
-    done(A.dma_start(T.fbd[:], T.fb[:]), "ld_fd", 16)
-    done(A.dma_start(T.fbo[:], T.fb[:]), "ld_fo", 16)
-    done(Y.dma_start(T.kt[:], T.k[:]), "ld_k", 16)
+    def send(left, *moves):
+        ts = []
+        for dst, engines, sem, src, to in moves:
+            rid, pid = topo.addr(dst, core)
+            ts.append(RemoteDMATransfer(dst_ids=[DstId(rid=rid, pnc=pid)], dma_engine_mask=bits(engines), remote_sem=S[sem], src=src, dst=to))
+            n[left] = n.get(left, 0) + len(engines)
+        g.remote_dma_fused(ts, local_sem=S[left])
 
-    done(g.iota(T.im[:], [[-16, 2], [0, 2], [-1, 16]], 64, 1), "k0")
-    done(V.memset(T.ones[:], 1.0), "k1")
-    done(V.memset(T.keep[:], 1.0), "k1")
-    need(V, "k1")
-    done(V.tensor_tensor_scan(T.num[:], T.ones[:], T.ones[:], -1.0, OP.add, OP.mult), "k2")
-    done(V.memset(T.keep[:, 0:128:32], 0.0), "k2")
-    need(V, "ld_a")
-    done(V.quantize_mx(T.qa[:], T.qas[:], T.at[:]), "qa_ok")
-    need(V, "k0")
-    done(V.tensor_scalar(T.am[:], T.im[:], 31, None, OP.bitwise_and), "k3")
-    need(V, "k3")
-    done(V.tensor_scalar(T.mask[:], T.am[:], 0.0, 4.0, OP.is_equal, OP.mult), "k4")
+    def constants():
+        done(g.iota(T.im[:], [[-16, 2], [0, 2], [-1, 16]], 64, 1), "k0")
+        done(V.memset(T.keep[:], 1.0), "k1")
+        done(V.memset(T.ones[:], 1.0), "k1")
+        need(V, "k1")
+        done(V.tensor_tensor_scan(T.num[:], T.ones[:], T.ones[:], -1.0, OP.add, OP.mult), "k2")
+        done(V.memset(T.keep[:, 0:64:32], 0.0), "k2")
+        need(V, "k0")
+        done(V.tensor_scalar(T.am[:], T.im[:], 31, None, OP.bitwise_and), "k3")
+        need(V, "k3")
+        done(V.tensor_scalar(T.mask[:], T.am[:], 0.0, 4.0, OP.is_equal, OP.mult), "k4")
+        need(V, "k2", "k4")
 
-    far = topo.engines(core, T.cores[mate])
-    chip = topo.engines(core, relay[(rank, cross[0])])
-    rest = [e for e in chip if e not in far]
+    def penalties(first):
+        for h in (0, 1):
+            done(V.tensor_scalar(T.fn[:, 4 * h:4 * h + 2], T.lf[:, 0:2], float(first + 256 * h), None, OP.subtract), "fn_ok")
+        need(V, "fn_ok")
+        need(A, "fn_ok", "k2")
+        for h in (0, 1):
+            c = slice(256 * h, 256 * h + 256)
+            done(V.tensor_scalar(T.pen0[:, c], T.num[:], T.fn[:, 4 * h:4 * h + 1], FAR, OP.is_equal, OP.mult), "pen_ok0")
+            done(A.activation(T.ab[:, c], T.num[:], ACT.Abs, bias=T.fn[:, 4 * h + 1:4 * h + 2], scale=-1.0), "ab_ok")
+        need(A, "ab_ok")
+        done(A.activation(T.pen1[:], T.ab[:], ACT.Relu, bias=FAR, scale=-FAR), "pen_ok1")
 
-    def xfer(dst, mask, sem, src, to):
-        rid, pid = topo.addr(dst, core)
-        return RemoteDMATransfer(dst_ids=[DstId(rid=rid, pnc=pid)], dma_engine_mask=mask, remote_sem=S[sem], src=src, dst=to)
-
-    def fused(sem, *ts):
-        g.remote_dma_fused(list(ts), local_sem=S[sem])
-
-    rl = [relay[(rank, d)] for d in cross]
-    dm = T.cores[mate]
-    half = [bits(chip[1::2]), bits(chip[0::2])]
-    need(g, "ld_fd")
-    fused("sf",
-          xfer(rl[0], bits(rest[0:2]), "rf_in", T.fbd[:], T.rfb[:]),
-          xfer(rl[1], bits(rest[2:4]), "rf_in", T.fbd[:], T.rfb[:]),
-          xfer(dm, bits(far[0::2]), "f_in%d" % rank, T.fbd[:], T.lf[:, rank:rank + 1]))
-    n["sf"] = 2 + 2 + len(far[0::2])
-    need(g, "qa_ok")
-    fused("sx",
-          xfer(rl[0], half[0], "rac_in", u8(T.qa[:]), u8(T.rac[:])),
-          xfer(rl[1], half[1], "rac_in", u8(T.qa[:]), u8(T.rac[:])))
-    fused("sx",
-          xfer(rl[0], half[0], "ras_in", T.qas[:], T.ras[:]),
-          xfer(rl[1], half[1], "ras_in", T.qas[:], T.ras[:]))
-    n["sx"] = 2 * len(chip)
-    rid, pid = topo.addr(dm, core)
-    s = slice(128 * rank, 128 * rank + 128)
-    g.remote_dma(u8(T.la[:, s]), u8(T.qa[:]), S["a_in%d" % rank], S.sp, pid, rid, bits(far))
-    g.remote_dma(T.las[:, s], T.qas[:], S["a_in%d" % rank], S.sp, pid, rid, bits(far))
-    n["sp"] = 2 * len(far)
-
-    need(Y, "sx")
-    done(Y.dma_start(T.vt[:], T.v[:]), "ld_v", 16)
-    done(Y.dma_start(T.ut[:], T.u[:]), "ld_u", 16)
-
-    for i in (1, 2, 3):
-        q = order[i]
-        last = T.cores[q] if (q, rank) not in relay else relay[(q, rank)]
-        e = len(topo.engines(last, core))
-        n["a_in%d" % q] = 2 * e
-        n["z_in%d" % q] = 2 * e
-        n["b_in%d" % q] = e
-        n["f_in%d" % q] = e if i > 1 else len(topo.engines(last, core)[0::2])
-        if i > 1:
-            n["lc_in"] = n["ln_in"] = e
-
-    def forbidden(i):
-        q = order[i]
-        if i == 0:
-            need(V, "ld_fo")
-            src = T.fbo[:]
-        else:
-            need(V, "f_in%d" % q)
-            src = T.lf[:, q:q + 1]
-        done(V.tensor_scalar(T["fn%d" % i][:], src, float(512 * rank), None, OP.subtract), "fn_ok%d" % i)
-
-    def pen_v(i):
-        need(V, "fn_ok%d" % i, "k2")
-        done(V.tensor_scalar(T["pen%d" % i][:], T.num[:], T["fn%d" % i][:], FAR, OP.is_equal, OP.mult), "pen_ok%d" % i)
-
-    def pen_a(i):
-        need(A, "fn_ok%d" % i, "k2")
-        done(A.activation(T["ab%d" % i][:], T.num[:], ACT.Abs, bias=T["fn%d" % i][:], scale=-1.0), "ab_ok%d" % i)
-        need(A, "ab_ok%d" % i)
-        done(A.activation(T["pen%d" % i][:], T["ab%d" % i][:], ACT.Relu, bias=FAR, scale=-FAR), "pen_ok%d" % i)
-
-    def anchors(i):
-        q = order[i]
-        if i == 0:
-            need(P, "qa_ok", "qk_ok")
-            return T.qa[:], T.qas[:]
-        need(P, "a_in%d" % q)
-        return T.la[:, 128 * q:128 * q + 128], T.las[:, 128 * q:128 * q + 128]
-
-    def score(i):
-        l, ls = anchors(i)
-        done(P.matmul_mx(T.ps[:, 512 * i:512 * i + 512], l, ls, T.qk[:], T.qks[:], True, True), "mm_ok%d" % i)
-
-    def halves(i):
-        l, ls = anchors(i)
-        done(P.matmul_mx(T.ps[:, 512 * i:512 * i + 256], l, ls, T.qk[:, 0:256], T.qks[:, 0:256], True, True), "mm_ok%d" % i)
-        done(P.matmul_mx(T.pu[:, 512 * i:512 * i + 256], l, ls, T.qk[:, 256:512], T.qks[:, 256:512], True, True), "half%d" % i)
-
-    def top(i):
-        m, r, p = T["ms%d" % i], T["run%d" % i], T["pen%d" % i]
-        need(V, "pen_ok%d" % i, "mm_ok%d" % i)
-        if i == 2:
-            done(V.tensor_tensor(m[:, 0:256], T.ps[:, 512 * i:512 * i + 256], p[:, 0:256], OP.subtract), "ms_ok%d" % i)
-            need(V, "half%d" % i)
-            done(V.tensor_tensor(m[:, 256:512], T.pu[:, 512 * i:512 * i + 256], p[:, 256:512], OP.subtract), "ms_ok%d" % i)
-        else:
-            done(V.tensor_tensor(m[:], T.ps[:, 512 * i:512 * i + 512], p[:], OP.subtract), "ms_ok%d" % i)
+    def search(i, anchors, scales, q, qs, lower, upper):
+        p, m, r = T["pen%d" % i], T["ms%d" % i], T["run%d" % i]
+        for h, ready, sem in ((0, lower, "mm_ok%d" % i), (1, upper, "half%d" % i)):
+            c, k = slice(256 * h, 256 * h + 256), slice(128 + 256 * h, 384 + 256 * h)
+            bank = T.ps[:, 1024 * i + 512 * h:1024 * i + 512 * h + 256]
+            need(P, *ready)
+            done(P.matmul_mx(bank, anchors, scales, q[:, k], qs[:, k], True, True), sem)
+            need(V, "pen_ok%d" % i, sem)
+            done(V.tensor_tensor(m[:, c], bank, p[:, c], OP.subtract), "ms_ok%d" % i)
         need(V, "ms_ok%d" % i)
         done(V.tensor_tensor_scan(r[:, 0:512], m[:], m[:], -FAR, OP.max, OP.max), "run_ok%d" % i)
         need(A, "run_ok%d" % i)
-        done(A.activation(T["sink%d" % i][:], r[:, 0:512], ACT.Sign, bias=r[:, 511:512], scale=-1.0,
-                          accum_out=r[:, 512:513]), "idx_ok%d" % i)
+        done(A.activation(T["sink%d" % i][:], r[:, 0:512], ACT.Sign, bias=r[:, 511:512], scale=-1.0, accum_out=r[:, 512:513]), "idx_ok%d" % i)
 
-    forbidden(0)
-    pen_v(0)
-    need(V, "ld_k")
-    done(V.quantize_mx(T.qk[:], T.qks[:], T.kt[:]), "qk_ok")
-    score(0)
-    top(0)
-    forbidden(1)
-    pen_v(1)
-    forbidden(2)
-    forbidden(3)
-    pen_a(2)
-    pen_a(3)
-    score(1)
-    top(1)
-    halves(2)
-    score(3)
-    top(2)
-    top(3)
+    def turn(l, idx, ready, scale):
+        c = slice(64 * l, 64 * l + 64)
+        need(V, ready)
+        done(V.tensor_scalar(T.x[:, c], T.mask[:], idx, scale, OP.mult, OP.mult), "x_ok%d" % l)
+        need(V, "x_ok%d" % l)
+        done(V.transpose(T.xt[:, c], T.x[:, c]), "xt_ok%d" % l)
+        need(V, "xt_ok%d" % l)
+        for a in range(4):
+            b = slice(32 * a, 32 * a + 32)
+            done(V.tensor_tensor_scan(T.xw[0:32, 256 * l + 64 * a:256 * l + 64 * a + 64], T.keep[b, :], T.xt[b, c], 0.0, OP.mult, OP.add),
+                 "xw_ok%d" % l)
 
-    need(g, "idx_ok1", "idx_ok2", "idx_ok3")
-    slot = T.best[:, 4 * rank:4 * rank + 2]
-    fused("sb",
-          xfer(rl[0], bits(rest[1::2]), "rb_in", T.run2[:, 511:513], T.rbest[:]),
-          xfer(rl[1], bits(rest[0::2]), "rb_in", T.run3[:, 511:513], T.rbest[:]),
-          xfer(dm, bits(far), "b_in%d" % rank, T.run1[:, 511:513], slot))
-    n["sb"] = len(rest) + len(far)
+    def spread(l0, l1):
+        need(V, *["xw_ok%d" % l for l in range(l0, l1)])
+        for a in range(4):
+            done(V.tensor_copy(T.off[32 * a:32 * a + 32, 8 * l0:8 * l1], T.xw[0:32, 256 * l0 + 31:256 * l1:32]), "off_ok%d" % l0)
 
-    def values(j, i0, i1):
-        x, xt, xw, o, z = T["x%d" % j], T["xt%d" % j], T["xw%d" % j], T["off%d" % j], T["z%d" % j]
-        for l, i in enumerate((i0, i1)):
-            need(V, "idx_ok%d" % i, "k4")
-            done(V.tensor_scalar(x[:, 64 * l:64 * l + 64], T.mask[:], T["run%d" % i][:, 512:513], None, OP.mult), "x_ok%d" % j)
-        need(V, "x_ok%d" % j)
-        done(V.transpose(xt[:], x[:]), "xt_ok%d" % j)
-        need(V, "xt_ok%d" % j)
-        done(V.tensor_tensor_scan(xw[:], T.keep[:], xt[:], 0.0, OP.mult, OP.add), "xw_ok%d" % j)
-        need(V, "xw_ok%d" % j)
-        for c in range(4):
-            b = 2 * (c % 2) + c // 2
-            for to in (c, c ^ 1):
-                done(V.tensor_copy(o[32 * to:32 * to + 32, b:16:4], xw[32 * c:32 * c + 32, 31:128:32]), "o1_ok%d" % j)
-        need(V, "o1_ok%d" % j)
-        done(V.tensor_copy(o[0:64, 1:16:2], o[64:128, 1:16:2]), "o2_ok%d" % j)
-        done(V.tensor_copy(o[64:128, 0:16:2], o[0:64, 0:16:2]), "o2_ok%d" % j)
-        need(V, "o2_ok%d" % j, "ld_v")
-        need(A, "o2_ok%d" % j, "ld_v")
-        for t in (0, 1):
-            done(V.tensor_copy(z[:, t:1024:4], T.vt[:, t:2048].indirect(o[:, 0:16])), "zv_ok%d" % j)
-        for t in (2, 3):
-            done(A.activation(z[:, t:1024:4], T.vt[:, t:2048].indirect(o[:, 0:16]), ACT.Copy), "zs_ok%d" % j)
-        need(V, "zv_ok%d" % j, "zs_ok%d" % j)
-        done(V.quantize_mx(T["zq%d" % j][:], T["zqs%d" % j][:], z[:]), "zq_ok%d" % j)
+    return n, done, need, send, constants, penalties, search, turn, spread
 
-    values(0, 2, 3)
-    need(g, "zq_ok0")
-    fused("sz",
-          xfer(rl[0], half[0], "rzc_in", u8(T.zq0[:, 0:128]), u8(T.rzc[:])),
-          xfer(rl[1], half[1], "rzc_in", u8(T.zq0[:, 128:256]), u8(T.rzc[:])))
-    fused("sz",
-          xfer(rl[0], half[0], "rzs_in", T.zqs0[:, 0:128], T.rzs[:]),
-          xfer(rl[1], half[1], "rzs_in", T.zqs0[:, 128:256], T.rzs[:]))
-    values(1, 1, 0)
-    need(g, "zq_ok1")
-    g.remote_dma(u8(T.lz[:, s]), u8(T.zq1[:, 0:128]), S["z_in%d" % rank], S.sz, pid, rid, bits(far))
-    g.remote_dma(T.lzs[:, s], T.zqs1[:, 0:128], S["z_in%d" % rank], S.sz, pid, rid, bits(far))
-    n["sz"] = 2 * len(chip) + 2 * len(far)
 
-    need(V, "ld_u")
+def rank_program(g, core, T, topo):
+    rank = T.rank_of(core)
+    if rank is None:
+        for r in range(len(T.cores)):
+            t = team(T, topo, r)
+            for job in JOBS:
+                if t[job] == core:
+                    (helper_program if job == "helper" else relay_program)(g, core, T, topo, r, t, job)
+        return
+    N = len(T.cores)
+    t = team(T, topo, rank)
+    V, P, A, Y = g.vector, g.tensor, g.scalar, g.sync
+    n, done, need, send, constants, penalties, search, turn, spread = tools(g, core, T, topo)
+    dm = T.cores[t["ranks"][D_]]
+    dh = team(T, topo, t["ranks"][D_])["helper"]
+    out = topo.engines(core, dm)
+    chip = topo.engines(core, t["helper"])
+    rest = [e for e in chip if e not in out]
+    r1, r2 = rest[:len(rest) // 2], rest[len(rest) // 2:]
+    col = [slice(128 * i, 128 * i + 128) for i in range(3)]
+    qa, qas = T.qx[:, 0:128], T.qxs[:, 0:128]
+
+    for i in range(3):
+        n["a_in%d" % i] = n["z_in%d" % i] = 2 * len(out)
+        n["b_in%d" % i] = len(out)
+        n["f_in%d" % i] = len(out) // 2
+    n["pos_in"] = n["ln_in"] = n["own_in"] = n["lo_in"] = len(out)
+
+    done(Y.dma_start(T.at[:], T.an[:]), "ld_a", 16)
+    done(A.dma_start(T.fbd[:], T.fb[:]), "ld_fd", 16)
+    for h in (0, 1):
+        done(Y.dma_start(T.kt[:, 1024 * h:1024 * h + 1024], T.k[:, 1024 * h:1024 * h + 1024]), "ld_k%d" % h, 16)
+    constants()
+    need(V, "ld_a")
+    done(V.quantize_mx(qa, qas, T.at[:]), "qa_ok")
+
+    need(g, "ld_fd")
+    send("sf", (t["scales"], r1, "rf_in", T.fbd[:], T.rfb[:]), (t["helper"], r2, "rf_in", T.fbd[:], T.rfb[:]),
+         (dh, out, "rd_in", T.fbd[:], T.rfd[:]))
+    need(g, "qa_ok")
+    send("sx", (t["codes"], chip, "ra_in", u8(qa), u8(T.rac[:])))
+    send("sx", (t["scales"], chip, "ra_in", qas, T.ras[:]))
+    send("sx", (dh, out, "a_in%d" % D_, u8(qa), u8(T.la[:, 0:128])))
+    send("sx", (dh, out, "a_in%d" % D_, qas, T.las[:, 0:128]))
+    for h, c, e in ((0, slice(128, 384), rest), (1, slice(384, 640), chip)):
+        k = slice(128 + 256 * h, 384 + 256 * h)
+        need(V, "ld_k%d" % h)
+        done(V.quantize_mx(T.qx[:, k], T.qxs[:, k], T.kt[:, 1024 * h:1024 * h + 1024]), "qk_ok%d" % h)
+        need(g, "qk_ok%d" % h)
+        send("sk", (t["helper"], e, "hx_in%d" % h, u8(T.qx[:, c]), u8(T.hx[:, c])))
+        send("sk", (t["helper"], e, "hx_in%d" % h, T.qxs[:, c], T.hxs[:, c]))
+    send("sk", (t["helper"], chip, "ra_in", u8(qa), u8(T.hx[:, 0:128])))
+    send("sk", (t["helper"], chip, "ra_in", qas, T.hxs[:, 0:128]))
+
+    need(Y, "sx", "qk_ok1")
+    done(Y.dma_start(T.vt[:], T.v[:]), "ld_v", 16)
+    done(Y.dma_start(T.ut[:], T.u[:]), "ld_u", 16)
+
+    need(V, "f_in%d" % A_, "f_in%d" % B_)
+    penalties(512 * rank)
+    for i in (A_, B_):
+        search(i, T.la[:, col[i]], T.las[:, col[i]], T.qx, T.qxs, ["qk_ok0", "a_in%d" % i], ["qk_ok1"])
+    for i in (A_, B_):
+        turn(i, T["run%d" % i][:, 512:513], "idx_ok%d" % i, 1.0)
+    spread(0, 2)
+
+    need(g, "idx_ok0", "idx_ok1")
+    send("sent", (t["scales2"], out, "rb_in", T.run0[:, 511:513], T.rbest[:]), (t["codes2"], rest, "rb_in", T.run1[:, 511:513], T.rbest[:]))
+
+    def values(i, o, ready):
+        z = T["z%d" % i]
+        need(V, ready, "ld_v")
+        need(A, ready, "ld_v")
+        for k in (0, 1):
+            done(V.tensor_copy(z[:, k:512:4], T.vt[:, k:2048].indirect(o)), "zv_ok%d" % i)
+        for k in (2, 3):
+            done(A.activation(z[:, k:512:4], T.vt[:, k:2048].indirect(o), ACT.Copy), "zs_ok%d" % i)
+        need(V, "zv_ok%d" % i, "zs_ok%d" % i)
+        done(V.quantize_mx(T["zq%d" % i][:], T["zqs%d" % i][:], z[:]), "zq_ok%d" % i)
+
+    for i, (c, s) in enumerate((("codes", "scales"), ("codes2", "scales2"))):
+        values(i, T.off[:, 8 * i:8 * i + 8], "off_ok0")
+        need(g, "zq_ok%d" % i)
+        send("sent", (t[c], chip, "rz_in", u8(T["zq%d" % i][:]), u8(T.rzc[:])))
+        send("sent", (t[s], chip, "rz_in", T["zqs%d" % i][:], T.rzs[:]))
+    values(D_, T.lo[:], "lo_in")
+    need(g, "zq_ok%d" % D_)
+    send("sent", (dm, out, "z_in%d" % D_, u8(T.zq2[:]), u8(T.lz[:, col[D_]])))
+    send("sent", (dm, out, "z_in%d" % D_, T.zqs2[:], T.lzs[:, col[D_]]))
+
+    place = [128 * q + (384 if q > rank else 0) for q in range(N)]
+    own = N - 1 - rank
+    need(V, "ld_u", "pos_in")
     done(V.quantize_mx(T.qu[:], T.qus[:], T.ut[:]), "qu_ok")
-    done(V.tensor_copy(slot, T.run0[:, 511:513]), "m1")
-    need(V, "m1", *["b_in%d" % q for q in order[1:]])
-    done(V.tensor_reduce(T.mx[:], T.best[:, 0:16:4], AxisListType.X, OP.max), "m2")
-    need(V, "m2")
-    done(V.tensor_scalar(T.t4[:], T.best[:, 0:16:4], T.mx[:], 4096.0, OP.is_lt, OP.mult), "m3")
-    need(V, "m3", "lc_in", "ln_in")
-    done(V.tensor_tensor(T.c1[:], T.t4[:], T.lc[:], OP.add), "m4")
-    done(V.tensor_tensor(T.c2[:], T.t4[:], T.ln[:], OP.add), "m4")
-    need(V, "m4")
-    done(V.tensor_reduce(T.pick[:], T.c1[:], AxisListType.X, OP.min), "pick_ok")
-    done(V.tensor_tensor(T.c3[:], T.c2[:], T.best[:, 1:16:4], OP.add), "m5")
-    need(V, "pick_ok", "m5")
-    done(V.tensor_scalar(T.xf[:], T.mask[:], T.pick[:], 0.25, OP.mult, OP.mult), "xf_ok")
-    done(V.tensor_reduce(T.won[:], T.c3[:], AxisListType.X, OP.min), "won_ok")
+    done(V.tensor_copy(T.pos[:], T.lp[:]), "m0")
+    done(V.quantize_mx(T.qv[:], T.qvs[:], T.vt[:]), "qv_ok")
+    need(V, "m0", "own_in", "ln_in", "b_in0", "b_in1", "b_in2")
+    done(V.tensor_reduce(T.mx[:], T.best[:, 0:16:4], AxisListType.X, OP.max), "m1")
+    done(V.tensor_scalar(T.pos[:, own:own + 1], T.best[:, 4 * own + 1:4 * own + 2], float(place[rank]), None, OP.add), "m2")
+    done(V.tensor_tensor(T.gl[:], T.best[:, 1:16:4], T.ln[:], OP.add), "m2")
+    need(V, "m1")
+    done(V.tensor_scalar(T.lt[:], T.best[:, 0:16:4], T.mx[:], None, OP.is_lt), "m3")
+    need(V, "m2", "m3")
+    done(V.tensor_tensor_scan(T.pick[:], T.lt[:], T.pos[:], 0.0, OP.mult, OP.max), "pick_ok")
+    done(V.tensor_tensor_scan(T.won[:], T.lt[:], T.gl[:], 0.0, OP.mult, OP.max), "won_ok")
     need(Y, "won_ok")
-    done(Y.dma_start(T.win[:], T.won[:]), "st", 16)
-    need(V, "xf_ok")
-    done(V.transpose(T.yf[:], T.xf[:]), "yf_ok")
-    need(V, "yf_ok")
-    done(V.tensor_tensor_scan(T.wf[:], T.keep[:, 0:64], T.yf[:], 0.0, OP.mult, OP.add), "wf_ok")
-    need(V, "wf_ok")
-    for c in range(4):
-        for to in (c, c ^ 1):
-            done(V.tensor_copy(T.of[32 * to:32 * to + 32, 2 * c:2 * c + 2], T.wf[32 * c:32 * c + 32, 31:64:32]), "of1_ok")
-    need(V, "of1_ok")
-    done(V.tensor_copy(T.of[0:64, 4:8], T.of[64:128, 4:8]), "of2_ok")
-    done(V.tensor_copy(T.of[64:128, 0:4], T.of[0:64, 0:4]), "of2_ok")
+    done(Y.dma_start(T.win[:], T.won[:, 3:4]), "st", 16)
+    turn(2, T.pick[:, 3:4], "pick_ok", 0.25)
+    spread(2, 3)
 
-    for i in range(4):
-        q = order[i]
-        if i == 0:
-            need(P, "qu_ok", "zq_ok1")
-            r, rs = T.zq1[:, 128:256], T.zqs1[:, 128:256]
-        else:
-            need(P, "z_in%d" % q)
-            r, rs = T.lz[:, 128 * q:128 * q + 128], T.lzs[:, 128 * q:128 * q + 128]
-        if i == 2:
-            need(P, "ms_ok2")
-        done(P.matmul_mx(T.pu[:, 512 * i:512 * i + 128], T.qu[:], T.qus[:], r, rs, True, True), "pu_ok%d" % i)
-        to, frm = T.prod[:, 128 * q:128 * q + 128], T.pu[:, 512 * i:512 * i + 128]
-        if i in (0, 2):
+    need(P, "qu_ok", "qv_ok")
+    done(P.matmul_mx(T.pu[:, 1536:2048], T.qu[:], T.qus[:], T.qv[:], T.qvs[:], True, True), "pu_ok3")
+    need(A, "pu_ok3")
+    done(A.activation(T.prod[:, place[rank]:place[rank] + 512], T.pu[:, 1536:2048], ACT.Copy), "us")
+    for i in (A_, D_, B_):
+        need(P, "z_in%d" % i)
+        done(P.matmul_mx(T.pu[:, 512 * i:512 * i + 128], T.qu[:], T.qus[:], T.lz[:, col[i]], T.lzs[:, col[i]], True, True), "pu_ok%d" % i)
+        q = t["ranks"][i]
+        to, frm = T.prod[:, place[q]:place[q] + 128], T.pu[:, 512 * i:512 * i + 128]
+        if i == B_:
             need(V, "pu_ok%d" % i)
             done(V.tensor_copy(to, frm), "uv")
         else:
             need(A, "pu_ok%d" % i)
             done(A.activation(to, frm, ACT.Copy), "us")
-    need(V, "of2_ok", "uv", "us")
-    done(V.tensor_copy(T.ysb[:], T.prod[:].indirect(T.of[:, 0:8])), "y_ok")
-    need(Y, "y_ok")
+    need(V, "off_ok2", "uv", "us")
+    need(A, "off_ok2", "uv", "us")
+    done(V.tensor_copy(T.ysb[:, 0:64], T.prod[:].indirect(T.off[:, 16:20])), "yv_ok")
+    done(A.activation(T.ysb[:, 64:128], T.prod[:].indirect(T.off[:, 20:24]), ACT.Copy), "ys_ok")
+    need(Y, "yv_ok", "ys_ok")
     done(Y.dma_start(T.y[:], T.ysb[:]), "st", 16)
     need(Y, "st")
-    need(g, "sf", "sp", "sb", "sz")
+    need(g, "sf", "sk", "sent")
 
 
-def relay_program(g, core, T, topo, r, d, place):
-    S = T.sem
+def helper_program(g, core, T, topo, r, t, job):
+    V, Y = g.vector, g.sync
+    n, done, need, send, constants, penalties, search, turn, spread = tools(g, core, T, topo)
+    me, dm = T.cores[r], T.cores[t["ranks"][D_]]
+    chip, out = topo.engines(core, me), topo.engines(core, dm)
+    n["rf_in"] = len(chip) // 4
+    n["rd_in"] = len(out)
+    n["a_in%d" % D_] = n["hx_in0"] = 2 * len(out)
+    n["hx_in1"] = n["ra_in"] = 2 * len(chip)
+    for i, sem, frm in ((1, "rf_in", T.rfb), (0, "rd_in", T.rfd)):
+        need(Y, sem)
+        done(Y.dma_start(T.lf[:, i:i + 1], frm[:]), "ld_f", 16)
+    constants()
+    need(V, "ld_f")
+    penalties(512 * r)
+    own = len(T.cores) - 1 - r
+    slot = T.best[:, 4 * own:4 * own + 2]
+    search(0, T.la[:, 0:128], T.las[:, 0:128], T.hx, T.hxs, ["hx_in0", "a_in%d" % D_], ["hx_in1"])
+    need(g, "idx_ok0")
+    send("sent", (dm, out, "b_in%d" % D_, T.run0[:, 511:513], slot))
+    turn(0, T.run0[:, 512:513], "idx_ok0", 1.0)
+    spread(0, 1)
+    need(g, "off_ok0")
+    send("sent", (me, [e for e in chip if e not in out], "lo_in", T.off[:, 0:8], T.lo[:]))
+    search(1, T.hx[:, 0:128], T.hxs[:, 0:128], T.hx, T.hxs, ["ra_in"], [])
+    need(g, "idx_ok1")
+    send("sent", (me, out, "own_in", T.run1[:, 511:513], slot))
+    need(g, "sent")
+
+
+def relay_program(g, core, T, topo, r, t, job):
     V = g.vector
-    dst = T.cores[d]
-    rid, pid = topo.addr(dst, core)
-    m = topo.mask(core, dst)
-    e = len(topo.engines(core, dst))
-    if place:
-        g.iota(T.ip[:], [[0, 4]], 0, 1).then_inc(S.k0, 1)
-        g.iota(T.cp[:], [[128, 4]], 0, 1, allow_small_or_imprecise_dtypes=True).then_inc(S.k0, 1)
-        V.wait_ge(S.k0, 2)
-        V.tensor_scalar(T.i1[:], T.ip[:], 4, 1, OP.arith_shift_right, OP.bitwise_and).then_inc(S.k3, 1)
-        V.tensor_scalar(T.i2[:], T.ip[:], 6, None, OP.arith_shift_right).then_inc(S.k3, 1)
-        V.wait_ge(S.k3, 2)
-        V.tensor_tensor(T.i3[:], T.i1[:], T.i2[:], OP.subtract).then_inc(S.k4, 1)
-        V.wait_ge(S.k4, 1)
-        V.tensor_scalar(T.cd[:], T.i3[:], 48.0, None, OP.mult).then_inc(S.k5, 1)
-        V.wait_ge(S.k5, 1)
-        V.tensor_tensor(T.cq[:], T.cp[:], T.cd[:], OP.add).then_inc(S.k1, 1)
-        g.wait_ge(S.k1, 1)
-        g.remote_dma(T.lc[:], T.cq[:], S.lc_in, S.rsent, pid, rid, m)
+    n, done, need, send = tools(g, core, T, topo)[:4]
+    N = len(T.cores)
+    me = T.cores[r]
+    to = [T.cores[q] for q in t["ranks"][:2]]
+    out = topo.engines(core, to[0])
+    chip = topo.engines(me, core)
+    col = [slice(128 * i, 128 * i + 128) for i in range(2)]
+    n["rf_in"] = len(chip) // 4
+    n["rb_in"] = len(chip) // 2
+    n["ra_in"] = n["rz_in"] = len(chip)
+    if job == "codes":
+        a = t["ranks"][A_]
+        done(g.iota(T.ci[:], [[-128, N]], 128 * (N - 1), 1), "k0")
+        need(V, "k0")
+        for q0, q1, more in ((0, a + 1, 0.0), (a + 1, N, 384.0)):
+            if q1 > q0:
+                done(V.tensor_scalar(T.cp[:, N - q1:N - q0], T.ci[:, N - q1:N - q0], more, None, OP.add), "k1")
+        need(g, "k1")
+        send("sent", (to[A_], out, "pos_in", T.cp[:], T.lp[:]))
+        need(g, "ra_in")
+        for i in (A_, B_):
+            send("sent", (to[i], out, "a_in%d" % i, u8(T.rac[:]), u8(T.la[:, col[i]])))
+    if job == "scales":
+        for q in range(N):
+            done(V.memset(T.cn[:, N - 1 - q:N - q], float(512 * q)), "k1")
+        need(g, "k1")
+        send("sent", (to[A_], out, "ln_in", T.cn[:], T.ln[:]))
+        need(g, "rf_in")
+        send("sent", *[(to[i], out[i::2], "f_in%d" % i, T.rfb[:], T.lf[:, i:i + 1]) for i in (A_, B_)])
+        need(g, "ra_in")
+        for i in (A_, B_):
+            send("sent", (to[i], out, "a_in%d" % i, T.ras[:], T.las[:, col[i]]))
+    i = A_ if job in ("codes", "scales") else B_
+    if job in ("codes2", "scales2"):
+        j = B_ if job == "codes2" else A_
+        need(g, "rb_in")
+        send("sent", (to[j], out, "b_in%d" % j, T.rbest[:], T.best[:, 4 * (N - 1 - r):4 * (N - 1 - r) + 2]))
+    need(g, "rz_in")
+    if job in ("codes", "codes2"):
+        send("sent", (to[i], out, "z_in%d" % i, u8(T.rzc[:]), u8(T.lz[:, col[i]])))
     else:
-        g.iota(T.nq[:], [[512, 4]], 0, 0, allow_small_or_imprecise_dtypes=True).then_inc(S.k0, 1)
-        g.wait_ge(S.k0, 1)
-        g.remote_dma(T.ln[:], T.nq[:], S.ln_in, S.rsent, pid, rid, m)
-    src = T.cores[r]
-    chip = topo.engines(src, core)
-    rest = [x for x in chip if x not in topo.engines(src, [c for i, c in enumerate(T.cores) if i != r and topo.may_write(src, c)][0])]
-    s = slice(128 * r, 128 * r + 128)
-    hops = [
-        ("rf_in", 2, T.lf[:, r:r + 1], T.rfb[:], "f_in"),
-        ("rac_in", len(chip) // 2, u8(T.la[:, s]), u8(T.rac[:]), "a_in"),
-        ("ras_in", len(chip) // 2, T.las[:, s], T.ras[:], "a_in"),
-        ("rb_in", len(rest) // 2, T.best[:, 4 * r:4 * r + 2], T.rbest[:], "b_in"),
-        ("rzc_in", len(chip) // 2, u8(T.lz[:, s]), u8(T.rzc[:]), "z_in"),
-        ("rzs_in", len(chip) // 2, T.lzs[:, s], T.rzs[:], "z_in"),
-    ]
-    for sem, k, to, frm, there in hops:
-        g.wait_ge(S[sem], k)
-        g.remote_dma(to, frm, S["%s%d" % (there, r)], S.rsent, pid, rid, m)
-    g.wait_ge(S.rsent, (1 + len(hops)) * e)
+        send("sent", (to[i], out, "z_in%d" % i, T.rzs[:], T.lzs[:, col[i]]))
+    need(g, "sent")

@@ -6,7 +6,8 @@ ACT = ActivationFunctionType
 C8 = "float8_e4m3fn_x4"
 FAR = 1.0e29
 A_, B_, D_ = 0, 1, 2
-JOBS = ("codes", "scales", "codes2", "scales2", "helper")
+JOBS = ("codes", "scales", "codes2", "helper")
+STEPS = "TA GA RA sA0 sA1 sA2 vA3 TB GB RB QA sB2 sB3 vB0 vB1 QB sD2 sD3 vD0 vD1 QD"
 
 SCRATCH = {
     "at": ("sbuf", [128, 512], "bfloat16"),
@@ -17,23 +18,23 @@ SCRATCH = {
     "qx": ("sbuf", [128, 640], C8), "qxs": ("sbuf", [128, 640], "uint8"),
     "qu": ("sbuf", [128, 128], C8), "qus": ("sbuf", [128, 128], "uint8"),
     "qv": ("sbuf", [128, 512], C8), "qvs": ("sbuf", [128, 512], "uint8"),
-    "la": ("sbuf", [128, 384], C8), "las": ("sbuf", [128, 384], "uint8"),
+    "la": ("sbuf", [128, 256], C8), "las": ("sbuf", [128, 256], "uint8"),
     "lf": ("sbuf", [128, 4], "int32"),
     "best": ("sbuf", [128, 16], "float32"),
     "lz": ("sbuf", [128, 384], C8), "lzs": ("sbuf", [128, 384], "uint8"),
-    "lp": ("sbuf", [128, 4], "uint16"), "ln": ("sbuf", [128, 4], "bfloat16"),
+    "lp": ("sbuf", [128, 1], "float32"), "ln": ("sbuf", [128, 4], "bfloat16"),
     "lo": ("sbuf", [128, 8], "uint16"),
-    "rfb": ("dram", [128, 1], "int32"), "rfd": ("dram", [128, 1], "int32"),
+    "rfb": ("dram", [128, 1], "int32"),
     "rac": ("sbuf", [128, 128], C8), "ras": ("sbuf", [128, 128], "uint8"),
     "rbest": ("sbuf", [128, 2], "float32"),
-    "rzc": ("sbuf", [128, 128], C8), "rzs": ("sbuf", [128, 128], "uint8"),
+    "rzc": ("sbuf", [128, 128], C8), "rzs": ("sbuf", [128, 256], "uint8"),
     "hx": ("sbuf", [128, 640], C8), "hxs": ("sbuf", [128, 640], "uint8"),
     "ones": ("sbuf", [128, 256], "bfloat16"),
     "num": ("sbuf", [128, 256], "bfloat16"),
     "im": ("sbuf", [128, 64], "int32"), "am": ("sbuf", [128, 64], "int32"),
     "mask": ("sbuf", [128, 64], "float32"),
     "keep": ("sbuf", [128, 64], "float32"),
-    "ci": ("sbuf", [128, 4], "int32"), "cp": ("sbuf", [128, 4], "uint16"), "cn": ("sbuf", [128, 4], "bfloat16"),
+    "cp": ("sbuf", [128, 1], "float32"), "cn": ("sbuf", [128, 4], "bfloat16"),
     "fn": ("sbuf", [128, 8], "float32"),
     "ab": ("sbuf", [128, 512], "bfloat16"),
     "x": ("sbuf", [128, 192], "float32"), "xt": ("sbuf", [128, 192], "float32"),
@@ -43,9 +44,9 @@ SCRATCH = {
     "pick": ("sbuf", [128, 4], "float32"), "won": ("sbuf", [128, 4], "float32"),
     "prod": ("sbuf", [128, 896], "float32"),
     "ysb": ("sbuf", [128, 128], "float32"),
-    "ps": ("psum", [128, 2048], "float32"),
-    "pu": ("psum", [128, 2048], "float32"),
 }
+for _i in range(8):
+    SCRATCH["p%d" % _i] = ("psum", [128, 512], "float32")
 for _i in range(2):
     SCRATCH["pen%d" % _i] = ("sbuf", [128, 512], "bfloat16")
     SCRATCH["ms%d" % _i] = ("sbuf", [128, 512], "float32")
@@ -59,10 +60,10 @@ for _i in range(3):
 SEMAPHORES = (
     ["ld_a", "ld_k0", "ld_k1", "ld_v", "ld_u", "ld_fd", "ld_f", "st"]
     + ["sf", "sx", "sk", "sent"]
-    + ["rf_in", "rd_in", "ra_in", "rb_in", "rz_in", "hx_in0", "hx_in1", "pos_in", "ln_in", "own_in", "lo_in"]
+    + ["rf_in", "rd_in", "ra_in", "rb_in", "rz_in", "rs_in0", "rs_in1", "hx_in0", "hx_in1", "pos_in", "ln_in", "own_in", "lo_in"]
     + ["%s%d" % (n, i) for n in ("a_in", "f_in", "b_in", "z_in") for i in range(3)]
     + ["k0", "k1", "k2", "k3", "k4", "qa_ok", "qk_ok0", "qk_ok1", "qu_ok", "qv_ok", "ab_ok", "fn_ok"]
-    + ["%s%d" % (n, i) for n in ("pen_ok", "mm_ok", "half", "ms_ok", "run_ok", "idx_ok") for i in range(2)]
+    + ["%s%d" % (n, i) for n in ("pen_ok", "mm0_ok", "mm1_ok", "mm2_ok", "ms0_ok", "ms1_ok", "ms2_ok", "run_ok", "idx_ok") for i in range(2)]
     + ["%s%d" % (n, i) for n in ("zv_ok", "zs_ok", "zq_ok", "x_ok", "xt_ok", "xw_ok", "off_ok") for i in range(3)]
     + ["pu_ok%d" % i for i in range(4)]
     + ["m0", "m1", "m2", "m3", "pick_ok", "won_ok", "uv", "us", "yv_ok", "ys_ok"]
@@ -90,7 +91,7 @@ def team(T, topo, r):
     near = [c for c in ports if topo.die(c) == topo.die(me)]
     far = [c for c in ports if c not in near]
     helper = [c for c in free if c not in ports and topo.die(c) == topo.die(me)][0]
-    return {"ranks": cross + direct, "codes": far[0], "scales": near[0], "codes2": far[1], "scales2": near[1], "helper": helper}
+    return {"ranks": cross + direct, "codes": far[0], "scales": near[0], "codes2": far[1], "helper": helper}
 
 
 def tools(g, core, T, topo):
@@ -126,12 +127,13 @@ def tools(g, core, T, topo):
         need(V, "k3")
         done(V.tensor_scalar(T.mask[:], T.am[:], 0.0, 4.0, OP.is_equal, OP.mult), "k4")
         need(V, "k2", "k4")
+        need(A, "k2", "k4")
 
     def penalties(first):
         for h in (0, 1):
             done(V.tensor_scalar(T.fn[:, 4 * h:4 * h + 2], T.lf[:, 0:2], float(first + 256 * h), None, OP.subtract), "fn_ok")
         need(V, "fn_ok")
-        need(A, "fn_ok", "k2")
+        need(A, "fn_ok")
         for h in (0, 1):
             c = slice(256 * h, 256 * h + 256)
             done(V.tensor_scalar(T.pen0[:, c], T.num[:], T.fn[:, 4 * h:4 * h + 1], FAR, OP.is_equal, OP.mult), "pen_ok0")
@@ -139,38 +141,52 @@ def tools(g, core, T, topo):
         need(A, "ab_ok")
         done(A.activation(T.pen1[:], T.ab[:], ACT.Relu, bias=FAR, scale=-FAR), "pen_ok1")
 
-    def search(i, anchors, scales, q, qs, lower, upper):
+    def search(i, anchors, scales, q, qs, pieces, early=False, between=None):
         p, m, r = T["pen%d" % i], T["ms%d" % i], T["run%d" % i]
-        for h, ready, sem in ((0, lower, "mm_ok%d" % i), (1, upper, "half%d" % i)):
-            c, k = slice(256 * h, 256 * h + 256), slice(128 + 256 * h, 384 + 256 * h)
-            bank = T.ps[:, 1024 * i + 512 * h:1024 * i + 512 * h + 256]
+
+        def running(c0, c1, *ready):
+            need(V, *ready)
+            done(V.tensor_tensor_scan(r[:, c0:c1], m[:, c0:c1], m[:, c0:c1], r[:, c0 - 1:c0] if c0 else -FAR, OP.max, OP.max), "run_ok%d" % i)
+
+        for h, (c0, c1, bank, ready) in enumerate(pieces):
+            c, k = slice(c0, c1), slice(128 + c0, 128 + c1)
             need(P, *ready)
-            done(P.matmul_mx(bank, anchors, scales, q[:, k], qs[:, k], True, True), sem)
-            need(V, "pen_ok%d" % i, sem)
-            done(V.tensor_tensor(m[:, c], bank, p[:, c], OP.subtract), "ms_ok%d" % i)
-        need(V, "ms_ok%d" % i)
-        done(V.tensor_tensor_scan(r[:, 0:512], m[:], m[:], -FAR, OP.max, OP.max), "run_ok%d" % i)
+            done(P.matmul_mx(bank[:, 0:c1 - c0], anchors, scales, q[:, k], qs[:, k], True, True), "mm%d_ok%d" % (h, i))
+            need(V, "pen_ok%d" % i, "mm%d_ok%d" % (h, i))
+            done(V.tensor_tensor(m[:, c], bank[:, 0:c1 - c0], p[:, c], OP.subtract), "ms%d_ok%d" % (h, i))
+            if early and h == 0:
+                running(0, 256, "ms0_ok%d" % i)
+        if between:
+            running(0, 256, "ms0_ok%d" % i)
+            between()
+        if early or between:
+            running(256, 512, "ms1_ok%d" % i, "run_ok%d" % i)
+        else:
+            running(0, 512, *["ms%d_ok%d" % (h, i) for h in range(len(pieces))])
         need(A, "run_ok%d" % i)
         done(A.activation(T["sink%d" % i][:], r[:, 0:512], ACT.Sign, bias=r[:, 511:512], scale=-1.0, accum_out=r[:, 512:513]), "idx_ok%d" % i)
+        need(A, "idx_ok%d" % i)
 
-    def turn(l, idx, ready, scale):
+    def masked(l, idx):
+        done(A.activation(T.x[:, 64 * l:64 * l + 64], T.mask[:], ACT.Identity, scale=idx), "x_ok%d" % l)
+
+    def turn(l, steps="TGR"):
         c = slice(64 * l, 64 * l + 64)
-        need(V, ready)
-        done(V.tensor_scalar(T.x[:, c], T.mask[:], idx, scale, OP.mult, OP.mult), "x_ok%d" % l)
-        need(V, "x_ok%d" % l)
-        done(V.transpose(T.xt[:, c], T.x[:, c]), "xt_ok%d" % l)
-        need(V, "xt_ok%d" % l)
-        for a in range(4):
-            b = slice(32 * a, 32 * a + 32)
-            done(V.tensor_tensor_scan(T.xw[0:32, 256 * l + 64 * a:256 * l + 64 * a + 64], T.keep[b, :], T.xt[b, c], 0.0, OP.mult, OP.add),
-                 "xw_ok%d" % l)
+        if "T" in steps:
+            need(V, "x_ok%d" % l)
+            done(V.transpose(T.xt[:, c], T.x[:, c]), "xt_ok%d" % l)
+        if "G" in steps:
+            need(V, "xt_ok%d" % l)
+            for a in range(4):
+                b = slice(32 * a, 32 * a + 32)
+                done(V.tensor_tensor_scan(T.xw[0:32, 256 * l + 64 * a:256 * l + 64 * a + 64], T.keep[b, :], T.xt[b, c], 0.0, OP.mult, OP.add),
+                     "xw_ok%d" % l)
+        if "R" in steps:
+            need(V, "xw_ok%d" % l)
+            for a in range(4):
+                done(V.tensor_copy(T.off[32 * a:32 * a + 32, 8 * l:8 * l + 8], T.xw[0:32, 256 * l + 31:256 * l + 256:32]), "off_ok%d" % l)
 
-    def spread(l0, l1):
-        need(V, *["xw_ok%d" % l for l in range(l0, l1)])
-        for a in range(4):
-            done(V.tensor_copy(T.off[32 * a:32 * a + 32, 8 * l0:8 * l1], T.xw[0:32, 256 * l0 + 31:256 * l1:32]), "off_ok%d" % l0)
-
-    return n, done, need, send, constants, penalties, search, turn, spread
+    return n, done, need, send, constants, penalties, search, masked, turn
 
 
 def rank_program(g, core, T, topo):
@@ -185,7 +201,7 @@ def rank_program(g, core, T, topo):
     N = len(T.cores)
     t = team(T, topo, rank)
     V, P, A, Y = g.vector, g.tensor, g.scalar, g.sync
-    n, done, need, send, constants, penalties, search, turn, spread = tools(g, core, T, topo)
+    n, done, need, send, constants, penalties, search, masked, turn = tools(g, core, T, topo)
     dm = T.cores[t["ranks"][D_]]
     dh = team(T, topo, t["ranks"][D_])["helper"]
     out = topo.engines(core, dm)
@@ -197,8 +213,7 @@ def rank_program(g, core, T, topo):
 
     for i in range(3):
         n["a_in%d" % i] = n["z_in%d" % i] = 2 * len(out)
-        n["b_in%d" % i] = len(out)
-        n["f_in%d" % i] = len(out) // 2
+        n["b_in%d" % i] = n["f_in%d" % i] = len(out)
     n["pos_in"] = n["ln_in"] = n["own_in"] = n["lo_in"] = len(out)
 
     done(Y.dma_start(T.at[:], T.an[:]), "ld_a", 16)
@@ -210,66 +225,68 @@ def rank_program(g, core, T, topo):
     done(V.quantize_mx(qa, qas, T.at[:]), "qa_ok")
 
     need(g, "ld_fd")
-    send("sf", (t["scales"], r1, "rf_in", T.fbd[:], T.rfb[:]), (t["helper"], r2, "rf_in", T.fbd[:], T.rfb[:]),
-         (dh, out, "rd_in", T.fbd[:], T.rfd[:]))
+    send("sf", (t["scales"], r1, "rf_in", T.fbd[:], T.rfb[:]), (t["codes"], r2, "rf_in", T.fbd[:], T.rfb[:]),
+         (t["helper"], out, "rf_in", T.fbd[:], T.rfb[:]))
     need(g, "qa_ok")
     send("sx", (t["codes"], chip, "ra_in", u8(qa), u8(T.rac[:])))
     send("sx", (t["scales"], chip, "ra_in", qas, T.ras[:]))
     send("sx", (dh, out, "a_in%d" % D_, u8(qa), u8(T.la[:, 0:128])))
     send("sx", (dh, out, "a_in%d" % D_, qas, T.las[:, 0:128]))
-    for h, c, e in ((0, slice(128, 384), rest), (1, slice(384, 640), chip)):
+    for h, e in ((0, rest), (1, chip)):
         k = slice(128 + 256 * h, 384 + 256 * h)
         need(V, "ld_k%d" % h)
         done(V.quantize_mx(T.qx[:, k], T.qxs[:, k], T.kt[:, 1024 * h:1024 * h + 1024]), "qk_ok%d" % h)
         need(g, "qk_ok%d" % h)
-        send("sk", (t["helper"], e, "hx_in%d" % h, u8(T.qx[:, c]), u8(T.hx[:, c])))
-        send("sk", (t["helper"], e, "hx_in%d" % h, T.qxs[:, c], T.hxs[:, c]))
-    send("sk", (t["helper"], chip, "ra_in", u8(qa), u8(T.hx[:, 0:128])))
-    send("sk", (t["helper"], chip, "ra_in", qas, T.hxs[:, 0:128]))
+        send("sk", (t["helper"], e, "hx_in%d" % h, u8(T.qx[:, k]), u8(T.hx[:, k])))
+        send("sk", (t["helper"], e, "hx_in%d" % h, T.qxs[:, k], T.hxs[:, k]))
 
     need(Y, "sx", "qk_ok1")
     done(Y.dma_start(T.vt[:], T.v[:]), "ld_v", 16)
     done(Y.dma_start(T.ut[:], T.u[:]), "ld_u", 16)
 
+    pieces = ([(0, 128, T.p0, ["qk_ok0", "a_in0"]), (128, 256, T.p1, []), (256, 512, T.p2, ["qk_ok1"])],
+              [(0, 256, T.p3, ["a_in1"]), (256, 512, T.p4, [])])
     need(V, "f_in%d" % A_, "f_in%d" % B_)
     penalties(512 * rank)
     for i in (A_, B_):
-        search(i, T.la[:, col[i]], T.las[:, col[i]], T.qx, T.qxs, ["qk_ok0", "a_in%d" % i], ["qk_ok1"])
-    for i in (A_, B_):
-        turn(i, T["run%d" % i][:, 512:513], "idx_ok%d" % i, 1.0)
-    spread(0, 2)
+        search(i, T.la[:, col[i]], T.las[:, col[i]], T.qx, T.qxs, pieces[i])
+        masked(i, T["run%d" % i][:, 512:513])
+        need(g, "idx_ok%d" % i)
+        send("sent", (t[("codes2", "scales")[i]], chip, "rb_in", T["run%d" % i][:, 511:513], T.rbest[:]))
 
-    need(g, "idx_ok0", "idx_ok1")
-    send("sent", (t["scales2"], out, "rb_in", T.run0[:, 511:513], T.rbest[:]), (t["codes2"], rest, "rb_in", T.run1[:, 511:513], T.rbest[:]))
-
-    def values(i, o, ready):
-        z = T["z%d" % i]
-        need(V, ready, "ld_v")
-        need(A, ready, "ld_v")
-        for k in (0, 1):
-            done(V.tensor_copy(z[:, k:512:4], T.vt[:, k:2048].indirect(o)), "zv_ok%d" % i)
-        for k in (2, 3):
-            done(A.activation(z[:, k:512:4], T.vt[:, k:2048].indirect(o), ACT.Copy), "zs_ok%d" % i)
+    lists = ((T.off[:, 0:8], "off_ok0"), (T.off[:, 8:16], "off_ok1"), (T.lo[:], "lo_in"))
+    for step in STEPS.split():
+        i = "ABD".index(step[1])
+        if step[0] in "TGR":
+            turn(i, step[0])
+            continue
+        if step[0] in "vs":
+            k = int(step[2])
+            to, frm = T["z%d" % i][:, k:512:4], T.vt[:, k:2048].indirect(lists[i][0])
+            need(V if step[0] == "v" else A, "ld_v", lists[i][1])
+            done(V.tensor_copy(to, frm) if step[0] == "v" else A.activation(to, frm, ACT.Copy), "z%s_ok%d" % (step[0], i))
+            continue
+        zq, zqs = T["zq%d" % i][:], T["zqs%d" % i][:]
         need(V, "zv_ok%d" % i, "zs_ok%d" % i)
-        done(V.quantize_mx(T["zq%d" % i][:], T["zqs%d" % i][:], z[:]), "zq_ok%d" % i)
-
-    for i, (c, s) in enumerate((("codes", "scales"), ("codes2", "scales2"))):
-        values(i, T.off[:, 8 * i:8 * i + 8], "off_ok0")
+        done(V.quantize_mx(zq, zqs, T["z%d" % i][:]), "zq_ok%d" % i)
         need(g, "zq_ok%d" % i)
-        send("sent", (t[c], chip, "rz_in", u8(T["zq%d" % i][:]), u8(T.rzc[:])))
-        send("sent", (t[s], chip, "rz_in", T["zqs%d" % i][:], T.rzs[:]))
-    values(D_, T.lo[:], "lo_in")
-    need(g, "zq_ok%d" % D_)
-    send("sent", (dm, out, "z_in%d" % D_, u8(T.zq2[:]), u8(T.lz[:, col[D_]])))
-    send("sent", (dm, out, "z_in%d" % D_, T.zqs2[:], T.lzs[:, col[D_]]))
+        if i == D_:
+            send("sent", (dm, out, "z_in%d" % D_, u8(zq), u8(T.lz[:, col[D_]])))
+            send("sent", (dm, out, "z_in%d" % D_, zqs, T.lzs[:, col[D_]]))
+        else:
+            send("sent", (t[("codes", "codes2")[i]], chip, "rz_in", u8(zq), u8(T.rzc[:])))
+            send("sent", (t["scales"], chip, "rs_in%d" % i, zqs, T.rzs[:, col[i]]))
 
     place = [128 * q + (384 if q > rank else 0) for q in range(N)]
     own = N - 1 - rank
-    need(V, "ld_u", "pos_in")
+    need(V, "ld_u", "pos_in", "ln_in")
+    done(V.tensor_scalar(T.pos[:], T.ln[:], 0.25, T.lp[:], OP.mult, OP.add), "m0")
     done(V.quantize_mx(T.qu[:], T.qus[:], T.ut[:]), "qu_ok")
-    done(V.tensor_copy(T.pos[:], T.lp[:]), "m0")
+    need(V, "m0")
+    if own > 0:
+        done(V.tensor_scalar(T.pos[:, 0:own], T.pos[:, 0:own], 384.0, None, OP.add), "m2")
     done(V.quantize_mx(T.qv[:], T.qvs[:], T.vt[:]), "qv_ok")
-    need(V, "m0", "own_in", "ln_in", "b_in0", "b_in1", "b_in2")
+    need(V, "own_in", "b_in0", "b_in1", "b_in2")
     done(V.tensor_reduce(T.mx[:], T.best[:, 0:16:4], AxisListType.X, OP.max), "m1")
     done(V.tensor_scalar(T.pos[:, own:own + 1], T.best[:, 4 * own + 1:4 * own + 2], float(place[rank]), None, OP.add), "m2")
     done(V.tensor_tensor(T.gl[:], T.best[:, 1:16:4], T.ln[:], OP.add), "m2")
@@ -280,18 +297,19 @@ def rank_program(g, core, T, topo):
     done(V.tensor_tensor_scan(T.won[:], T.lt[:], T.gl[:], 0.0, OP.mult, OP.max), "won_ok")
     need(Y, "won_ok")
     done(Y.dma_start(T.win[:], T.won[:, 3:4]), "st", 16)
-    turn(2, T.pick[:, 3:4], "pick_ok", 0.25)
-    spread(2, 3)
+    need(V, "pick_ok")
+    done(V.tensor_scalar(T.x[:, 128:192], T.mask[:], T.pick[:, 3:4], 0.25, OP.mult, OP.mult), "x_ok2")
+    turn(2)
 
     need(P, "qu_ok", "qv_ok")
-    done(P.matmul_mx(T.pu[:, 1536:2048], T.qu[:], T.qus[:], T.qv[:], T.qvs[:], True, True), "pu_ok3")
+    done(P.matmul_mx(T.p4[:], T.qu[:], T.qus[:], T.qv[:], T.qvs[:], True, True), "pu_ok3")
     need(A, "pu_ok3")
-    done(A.activation(T.prod[:, place[rank]:place[rank] + 512], T.pu[:, 1536:2048], ACT.Copy), "us")
+    done(A.activation(T.prod[:, place[rank]:place[rank] + 512], T.p4[:], ACT.Copy), "us")
     for i in (A_, D_, B_):
+        frm = T["p%d" % (5 + i)][:, 0:128]
+        to = T.prod[:, place[t["ranks"][i]]:place[t["ranks"][i]] + 128]
         need(P, "z_in%d" % i)
-        done(P.matmul_mx(T.pu[:, 512 * i:512 * i + 128], T.qu[:], T.qus[:], T.lz[:, col[i]], T.lzs[:, col[i]], True, True), "pu_ok%d" % i)
-        q = t["ranks"][i]
-        to, frm = T.prod[:, place[q]:place[q] + 128], T.pu[:, 512 * i:512 * i + 128]
+        done(P.matmul_mx(frm, T.qu[:], T.qus[:], T.lz[:, col[i]], T.lzs[:, col[i]], True, True), "pu_ok%d" % i)
         if i == B_:
             need(V, "pu_ok%d" % i)
             done(V.tensor_copy(to, frm), "uv")
@@ -310,29 +328,30 @@ def rank_program(g, core, T, topo):
 
 def helper_program(g, core, T, topo, r, t, job):
     V, Y = g.vector, g.sync
-    n, done, need, send, constants, penalties, search, turn, spread = tools(g, core, T, topo)
+    n, done, need, send, constants, penalties, search, masked, turn = tools(g, core, T, topo)
     me, dm = T.cores[r], T.cores[t["ranks"][D_]]
     chip, out = topo.engines(core, me), topo.engines(core, dm)
-    n["rf_in"] = len(chip) // 4
-    n["rd_in"] = len(out)
-    n["a_in%d" % D_] = n["hx_in0"] = 2 * len(out)
-    n["hx_in1"] = n["ra_in"] = 2 * len(chip)
-    for i, sem, frm in ((1, "rf_in", T.rfb), (0, "rd_in", T.rfd)):
-        need(Y, sem)
-        done(Y.dma_start(T.lf[:, i:i + 1], frm[:]), "ld_f", 16)
+    n["rf_in"] = n["rd_in"] = len(out)
+    n["a_in%d" % D_] = n["hx_in0"] = n["ra_in"] = 2 * len(out)
+    n["hx_in1"] = 2 * len(chip)
+    need(Y, "rf_in")
+    done(Y.dma_start(T.lf[:, 1:2], T.rfb[:]), "ld_f", 16)
     constants()
-    need(V, "ld_f")
+    need(g, "rf_in")
+    send("sent", (team(T, topo, t["ranks"][D_])["helper"], out, "rd_in", T.rfb[:], T.lf[:, 0:1]))
+    need(V, "ld_f", "rd_in")
     penalties(512 * r)
     own = len(T.cores) - 1 - r
     slot = T.best[:, 4 * own:4 * own + 2]
-    search(0, T.la[:, 0:128], T.las[:, 0:128], T.hx, T.hxs, ["hx_in0", "a_in%d" % D_], ["hx_in1"])
+    search(0, T.la[:, 0:128], T.las[:, 0:128], T.hx, T.hxs,
+           [(0, 256, T.p0, ["hx_in0", "a_in%d" % D_]), (256, 512, T.p1, ["hx_in1"])], True)
+    masked(0, T.run0[:, 512:513])
     need(g, "idx_ok0")
     send("sent", (dm, out, "b_in%d" % D_, T.run0[:, 511:513], slot))
-    turn(0, T.run0[:, 512:513], "idx_ok0", 1.0)
-    spread(0, 1)
+    turn(0)
     need(g, "off_ok0")
-    send("sent", (me, [e for e in chip if e not in out], "lo_in", T.off[:, 0:8], T.lo[:]))
-    search(1, T.hx[:, 0:128], T.hxs[:, 0:128], T.hx, T.hxs, ["ra_in"], [])
+    send("sent", (me, out, "lo_in", T.off[:, 0:8], T.lo[:]))
+    search(1, T.hx[:, 0:128], T.hxs[:, 0:128], T.hx, T.hxs, [(0, 512, T.p2, ["ra_in"])])
     need(g, "idx_ok1")
     send("sent", (me, out, "own_in", T.run1[:, 511:513], slot))
     need(g, "sent")
@@ -346,40 +365,41 @@ def relay_program(g, core, T, topo, r, t, job):
     to = [T.cores[q] for q in t["ranks"][:2]]
     out = topo.engines(core, to[0])
     chip = topo.engines(me, core)
+    rest = [e for e in chip if e not in out]
     col = [slice(128 * i, 128 * i + 128) for i in range(2)]
     n["rf_in"] = len(chip) // 4
-    n["rb_in"] = len(chip) // 2
-    n["ra_in"] = n["rz_in"] = len(chip)
+    n["ra_in"] = n["rb_in"] = n["rz_in"] = n["rs_in0"] = n["rs_in1"] = len(chip)
     if job == "codes":
-        a = t["ranks"][A_]
-        done(g.iota(T.ci[:], [[-128, N]], 128 * (N - 1), 1), "k0")
-        need(V, "k0")
-        for q0, q1, more in ((0, a + 1, 0.0), (a + 1, N, 384.0)):
-            if q1 > q0:
-                done(V.tensor_scalar(T.cp[:, N - q1:N - q0], T.ci[:, N - q1:N - q0], more, None, OP.add), "k1")
-        need(g, "k1")
+        done(g.iota(T.cp[:], [[0, 1]], 0, 1, allow_small_or_imprecise_dtypes=True), "k0")
+        need(g, "k0")
         send("sent", (to[A_], out, "pos_in", T.cp[:], T.lp[:]))
+        need(g, "rf_in")
+        send("sent", (to[B_], out, "f_in%d" % B_, T.rfb[:], T.lf[:, B_:B_ + 1]))
         need(g, "ra_in")
         for i in (A_, B_):
             send("sent", (to[i], out, "a_in%d" % i, u8(T.rac[:]), u8(T.la[:, col[i]])))
+        send("sent", (t["helper"], rest, "ra_in", u8(T.rac[:]), u8(T.hx[:, 0:128])))
     if job == "scales":
         for q in range(N):
             done(V.memset(T.cn[:, N - 1 - q:N - q], float(512 * q)), "k1")
         need(g, "k1")
         send("sent", (to[A_], out, "ln_in", T.cn[:], T.ln[:]))
         need(g, "rf_in")
-        send("sent", *[(to[i], out[i::2], "f_in%d" % i, T.rfb[:], T.lf[:, i:i + 1]) for i in (A_, B_)])
+        send("sent", (to[A_], out, "f_in%d" % A_, T.rfb[:], T.lf[:, A_:A_ + 1]))
         need(g, "ra_in")
         for i in (A_, B_):
             send("sent", (to[i], out, "a_in%d" % i, T.ras[:], T.las[:, col[i]]))
-    i = A_ if job in ("codes", "scales") else B_
-    if job in ("codes2", "scales2"):
-        j = B_ if job == "codes2" else A_
+        send("sent", (t["helper"], rest, "ra_in", T.ras[:], T.hxs[:, 0:128]))
+    if job != "codes":
+        i = A_ if job == "codes2" else B_
         need(g, "rb_in")
-        send("sent", (to[j], out, "b_in%d" % j, T.rbest[:], T.best[:, 4 * (N - 1 - r):4 * (N - 1 - r) + 2]))
-    need(g, "rz_in")
-    if job in ("codes", "codes2"):
-        send("sent", (to[i], out, "z_in%d" % i, u8(T.rzc[:]), u8(T.lz[:, col[i]])))
+        send("sent", (to[i], out, "b_in%d" % i, T.rbest[:], T.best[:, 4 * (N - 1 - r):4 * (N - 1 - r) + 2]))
+    if job == "scales":
+        for i in (A_, B_):
+            need(g, "rs_in%d" % i)
+            send("sent", (to[i], out, "z_in%d" % i, T.rzs[:, col[i]], T.lzs[:, col[i]]))
     else:
-        send("sent", (to[i], out, "z_in%d" % i, T.rzs[:], T.lzs[:, col[i]]))
+        i = A_ if job == "codes" else B_
+        need(g, "rz_in")
+        send("sent", (to[i], out, "z_in%d" % i, u8(T.rzc[:]), u8(T.lz[:, col[i]])))
     need(g, "sent")

@@ -7,7 +7,10 @@ C8 = "float8_e4m3fn_x4"
 FAR = 1.0e29
 A_, B_, D_ = 0, 1, 2
 JOBS = ("codes", "scales", "codes2", "helper")
-STEPS = "TA GA RA sA0 sA1 sA2 vA3 TB GB RB QA sB2 sB3 vB0 vB1 QB sD2 sD3 vD0 vD1 QD"
+STEPS = ("mA0 mA1 mA2 wA mB0 mB1 wB TA GA RA sA0 sA1 sA2 vA3 TB GB RB QA sB2 sB3 vB0 vB1 QB sD1 sD2 sD3 cU vD0 pV0 pV1 cX QD "
+         "cN cL pV2 cP pV3 cK cW TP cG GP RP")
+BACK = ([[("c", 0, 128, "codes")], [("s", 0, 128, "scales")]],
+        [[("c", 0, 64, "codes2"), ("c", 64, 128, "scales")], [("s", 0, 128, "codes")]])
 
 SCRATCH = {
     "at": ("sbuf", [128, 512], "bfloat16"),
@@ -27,18 +30,18 @@ SCRATCH = {
     "rfb": ("dram", [128, 1], "int32"),
     "rac": ("sbuf", [128, 128], C8), "ras": ("sbuf", [128, 128], "uint8"),
     "rbest": ("sbuf", [128, 2], "float32"),
-    "rzc": ("sbuf", [128, 128], C8), "rzs": ("sbuf", [128, 256], "uint8"),
+    "rz": ("sbuf", [128, 256], C8), "rzs": ("sbuf", [128, 256], "uint8"),
     "hx": ("sbuf", [128, 640], C8), "hxs": ("sbuf", [128, 640], "uint8"),
     "ones": ("sbuf", [128, 256], "bfloat16"),
     "num": ("sbuf", [128, 256], "bfloat16"),
-    "im": ("sbuf", [128, 64], "int32"), "am": ("sbuf", [128, 64], "int32"),
-    "mask": ("sbuf", [128, 64], "float32"),
+    "im": ("sbuf", [128, 32], "int32"), "am": ("sbuf", [128, 32], "int32"),
+    "mask": ("sbuf", [128, 32], "float32"),
     "keep": ("sbuf", [128, 64], "float32"),
     "cp": ("sbuf", [128, 1], "float32"), "cn": ("sbuf", [128, 4], "bfloat16"),
     "fn": ("sbuf", [128, 8], "float32"),
     "ab": ("sbuf", [128, 512], "bfloat16"),
     "x": ("sbuf", [128, 192], "float32"), "xt": ("sbuf", [128, 192], "float32"),
-    "xw": ("sbuf", [128, 768], "float32"), "off": ("sbuf", [128, 24], "uint16"),
+    "xw": ("sbuf", [128, 384], "float32"), "off": ("sbuf", [128, 24], "uint16"),
     "pos": ("sbuf", [128, 4], "float32"),
     "mx": ("sbuf", [128, 1], "float32"), "lt": ("sbuf", [128, 4], "float32"), "gl": ("sbuf", [128, 4], "float32"),
     "pick": ("sbuf", [128, 4], "float32"), "won": ("sbuf", [128, 4], "float32"),
@@ -55,18 +58,18 @@ for _i in range(2):
 for _i in range(3):
     SCRATCH["z%d" % _i] = ("sbuf", [128, 512], "bfloat16")
     SCRATCH["zq%d" % _i] = ("sbuf", [128, 128], C8)
-    SCRATCH["zqs%d" % _i] = ("sbuf", [128, 128], "uint8")
+    SCRATCH["zq%ds" % _i] = ("sbuf", [128, 128], "uint8")
 
 SEMAPHORES = (
     ["ld_a", "ld_k0", "ld_k1", "ld_v", "ld_u", "ld_fd", "ld_f", "st"]
     + ["sf", "sx", "sk", "sent"]
-    + ["rf_in", "rd_in", "ra_in", "rb_in", "rz_in", "rs_in0", "rs_in1", "hx_in0", "hx_in1", "pos_in", "ln_in", "own_in", "lo_in"]
+    + ["rf_in", "rd_in", "ra_in", "rb_in", "rc_in0", "rc_in1", "rs_in0", "rs_in1", "hx_in", "pos_in", "ln_in", "own_in", "lo_in"]
     + ["%s%d" % (n, i) for n in ("a_in", "f_in", "b_in", "z_in") for i in range(3)]
-    + ["k0", "k1", "k2", "k3", "k4", "qa_ok", "qk_ok0", "qk_ok1", "qu_ok", "qv_ok", "ab_ok", "fn_ok"]
+    + ["k0", "k1", "k2", "k3", "k4", "qa_ok", "qk_ok", "qu_ok", "ab_ok", "fn_ok"]
     + ["%s%d" % (n, i) for n in ("pen_ok", "mm0_ok", "mm1_ok", "mm2_ok", "ms0_ok", "ms1_ok", "ms2_ok", "run_ok", "idx_ok") for i in range(2)]
     + ["%s%d" % (n, i) for n in ("zv_ok", "zs_ok", "zq_ok", "x_ok", "xt_ok", "xw_ok", "off_ok") for i in range(3)]
-    + ["pu_ok%d" % i for i in range(4)]
-    + ["m0", "m1", "m2", "m3", "pick_ok", "won_ok", "uv", "us", "yv_ok", "ys_ok"]
+    + ["pu_ok%d" % i for i in range(8)] + ["qv_ok%d" % i for i in range(4)]
+    + ["m0", "m1", "m2", "m3", "m4", "pick_ok", "won_ok", "uv", "us", "yv_ok", "ys_ok"]
 )
 
 
@@ -79,6 +82,10 @@ def bits(engines):
 
 def u8(view):
     return view.bitcast(dt.uint8)
+
+
+def piece(T, name, kind, c0, c1):
+    return u8(T[name][:, c0:c1]) if kind == "c" else T[name + "s"][:, c0:c1]
 
 
 def team(T, topo, r):
@@ -116,77 +123,75 @@ def tools(g, core, T, topo):
         g.remote_dma_fused(ts, local_sem=S[left])
 
     def constants():
-        done(g.iota(T.im[:], [[-16, 2], [0, 2], [-1, 16]], 64, 1), "k0")
+        done(g.iota(T.im[:], [[0, 2], [-1, 16]], 16, 1), "k0")
         done(V.memset(T.keep[:], 1.0), "k1")
         done(V.memset(T.ones[:], 1.0), "k1")
         need(V, "k1")
         done(V.tensor_tensor_scan(T.num[:], T.ones[:], T.ones[:], -1.0, OP.add, OP.mult), "k2")
-        done(V.memset(T.keep[:, 0:64:32], 0.0), "k2")
+        done(V.memset(T.keep[:, 0:64:16], 0.0), "k2")
         need(V, "k0")
-        done(V.tensor_scalar(T.am[:], T.im[:], 31, None, OP.bitwise_and), "k3")
+        done(V.tensor_scalar(T.am[:], T.im[:], 15, None, OP.bitwise_and), "k3")
         need(V, "k3")
         done(V.tensor_scalar(T.mask[:], T.am[:], 0.0, 4.0, OP.is_equal, OP.mult), "k4")
         need(V, "k2", "k4")
         need(A, "k2", "k4")
 
-    def penalties(first):
+    def penalties(first, i, j=None):
+        e = i + 1 if j is None else j + 1
+        half = [slice(256 * h, 256 * h + 256) for h in (0, 1)]
         for h in (0, 1):
-            done(V.tensor_scalar(T.fn[:, 4 * h:4 * h + 2], T.lf[:, 0:2], float(first + 256 * h), None, OP.subtract), "fn_ok")
+            done(V.tensor_scalar(T.fn[:, 4 * h + i:4 * h + e], T.lf[:, i:e], float(first + 256 * h), None, OP.subtract), "fn_ok")
         need(V, "fn_ok")
-        need(A, "fn_ok")
         for h in (0, 1):
-            c = slice(256 * h, 256 * h + 256)
-            done(V.tensor_scalar(T.pen0[:, c], T.num[:], T.fn[:, 4 * h:4 * h + 1], FAR, OP.is_equal, OP.mult), "pen_ok0")
-            done(A.activation(T.ab[:, c], T.num[:], ACT.Abs, bias=T.fn[:, 4 * h + 1:4 * h + 2], scale=-1.0), "ab_ok")
-        need(A, "ab_ok")
-        done(A.activation(T.pen1[:], T.ab[:], ACT.Relu, bias=FAR, scale=-FAR), "pen_ok1")
+            done(V.tensor_scalar(T["pen%d" % i][:, half[h]], T.num[:], T.fn[:, 4 * h + i:4 * h + i + 1], FAR, OP.is_equal, OP.mult), "pen_ok%d" % i)
+        if j is not None:
+            need(A, "fn_ok")
+            for h in (0, 1):
+                done(A.activation(T.ab[:, half[h]], T.num[:], ACT.Abs, bias=T.fn[:, 4 * h + j:4 * h + j + 1], scale=-1.0), "ab_ok")
+            need(A, "ab_ok")
+            done(A.activation(T["pen%d" % j][:], T.ab[:], ACT.Relu, bias=FAR, scale=-FAR), "pen_ok%d" % j)
 
-    def search(i, anchors, scales, q, qs, pieces, early=False, between=None):
-        p, m, r = T["pen%d" % i], T["ms%d" % i], T["run%d" % i]
+    def scores(i, h, anchors, scales, q, qs, c0, c1, bank, ready):
+        c, k = slice(c0, c1), slice(128 + c0, 128 + c1)
+        need(P, *ready)
+        done(P.matmul_mx(bank[:, 0:c1 - c0], anchors, scales, q[:, k], qs[:, k], True, True), "mm%d_ok%d" % (h, i))
+        need(V, "pen_ok%d" % i, "mm%d_ok%d" % (h, i))
+        done(V.tensor_tensor(T["ms%d" % i][:, c], bank[:, 0:c1 - c0], T["pen%d" % i][:, c], OP.subtract), "ms%d_ok%d" % (h, i))
 
-        def running(c0, c1, *ready):
-            need(V, *ready)
-            done(V.tensor_tensor_scan(r[:, c0:c1], m[:, c0:c1], m[:, c0:c1], r[:, c0 - 1:c0] if c0 else -FAR, OP.max, OP.max), "run_ok%d" % i)
+    def running(i, c0, c1, pieces):
+        m, r = T["ms%d" % i], T["run%d" % i]
+        need(V, *["ms%d_ok%d" % (h, i) for h in pieces])
+        if c0:
+            need(V, "run_ok%d" % i)
+        done(V.tensor_tensor_scan(r[:, c0:c1], m[:, c0:c1], m[:, c0:c1], r[:, c0 - 1:c0] if c0 else -FAR, OP.max, OP.max), "run_ok%d" % i)
+        if c1 == 512:
+            need(A, "run_ok%d" % i)
+            done(A.activation(T["sink%d" % i][:], r[:, 0:512], ACT.Sign, bias=r[:, 511:512], scale=-1.0, accum_out=r[:, 512:513]), "idx_ok%d" % i)
 
-        for h, (c0, c1, bank, ready) in enumerate(pieces):
-            c, k = slice(c0, c1), slice(128 + c0, 128 + c1)
-            need(P, *ready)
-            done(P.matmul_mx(bank[:, 0:c1 - c0], anchors, scales, q[:, k], qs[:, k], True, True), "mm%d_ok%d" % (h, i))
-            need(V, "pen_ok%d" % i, "mm%d_ok%d" % (h, i))
-            done(V.tensor_tensor(m[:, c], bank[:, 0:c1 - c0], p[:, c], OP.subtract), "ms%d_ok%d" % (h, i))
-            if early and h == 0:
-                running(0, 256, "ms0_ok%d" % i)
-        if between:
-            running(0, 256, "ms0_ok%d" % i)
-            between()
-        if early or between:
-            running(256, 512, "ms1_ok%d" % i, "run_ok%d" % i)
-        else:
-            running(0, 512, *["ms%d_ok%d" % (h, i) for h in range(len(pieces))])
-        need(A, "run_ok%d" % i)
-        done(A.activation(T["sink%d" % i][:], r[:, 0:512], ACT.Sign, bias=r[:, 511:512], scale=-1.0, accum_out=r[:, 512:513]), "idx_ok%d" % i)
-        need(A, "idx_ok%d" % i)
+    def masked(l):
+        need(A, "idx_ok%d" % l)
+        for h in (0, 1):
+            p, c = slice(64 * h, 64 * h + 64), slice(64 * l + 32 * h, 64 * l + 32 * h + 32)
+            done(A.activation(T.x[0:64, c], T.mask[p, :], ACT.Identity, scale=T["run%d" % l][p, 512:513]), "x_ok%d" % l)
 
-    def masked(l, idx):
-        done(A.activation(T.x[:, 64 * l:64 * l + 64], T.mask[:], ACT.Identity, scale=idx), "x_ok%d" % l)
-
-    def turn(l, steps="TGR"):
-        c = slice(64 * l, 64 * l + 64)
+    def turn(l, steps="TGR", blocks=2):
+        w = 128 // blocks
+        c = slice(64 * l, 64 * l + w)
         if "T" in steps:
             need(V, "x_ok%d" % l)
-            done(V.transpose(T.xt[:, c], T.x[:, c]), "xt_ok%d" % l)
+            done(V.transpose(T.xt[0:32 * blocks, c], T.x[0:32 * blocks, c]), "xt_ok%d" % l)
         if "G" in steps:
             need(V, "xt_ok%d" % l)
-            for a in range(4):
+            for a in range(blocks):
                 b = slice(32 * a, 32 * a + 32)
-                done(V.tensor_tensor_scan(T.xw[0:32, 256 * l + 64 * a:256 * l + 64 * a + 64], T.keep[b, :], T.xt[b, c], 0.0, OP.mult, OP.add),
+                done(V.tensor_tensor_scan(T.xw[0:32, 128 * l + w * a:128 * l + w * a + w], T.keep[b, 0:w], T.xt[b, c], 0.0, OP.mult, OP.add),
                      "xw_ok%d" % l)
         if "R" in steps:
             need(V, "xw_ok%d" % l)
             for a in range(4):
-                done(V.tensor_copy(T.off[32 * a:32 * a + 32, 8 * l:8 * l + 8], T.xw[0:32, 256 * l + 31:256 * l + 256:32]), "off_ok%d" % l)
+                done(V.tensor_copy(T.off[32 * a:32 * a + 32, 8 * l:8 * l + 8], T.xw[0:32, 128 * l + 15:128 * l + 128:16]), "off_ok%d" % l)
 
-    return n, done, need, send, constants, penalties, search, masked, turn
+    return n, done, need, send, constants, penalties, scores, running, masked, turn
 
 
 def rank_program(g, core, T, topo):
@@ -201,23 +206,24 @@ def rank_program(g, core, T, topo):
     N = len(T.cores)
     t = team(T, topo, rank)
     V, P, A, Y = g.vector, g.tensor, g.scalar, g.sync
-    n, done, need, send, constants, penalties, search, masked, turn = tools(g, core, T, topo)
+    n, done, need, send, constants, penalties, scores, running, masked, turn = tools(g, core, T, topo)
     dm = T.cores[t["ranks"][D_]]
     dh = team(T, topo, t["ranks"][D_])["helper"]
     out = topo.engines(core, dm)
     chip = topo.engines(core, t["helper"])
     rest = [e for e in chip if e not in out]
-    r1, r2 = rest[:len(rest) // 2], rest[len(rest) // 2:]
     col = [slice(128 * i, 128 * i + 128) for i in range(3)]
     qa, qas = T.qx[:, 0:128], T.qxs[:, 0:128]
 
     for i in range(3):
         n["a_in%d" % i] = n["z_in%d" % i] = 2 * len(out)
-        n["b_in%d" % i] = n["f_in%d" % i] = len(out)
+        n["b_in%d" % i], n["f_in%d" % i] = len(out), len(out) // 2
+    for i in (A_, B_):
+        n["z_in%d" % i] = len(out) * sum(len(call) for call in BACK[i])
     n["pos_in"] = n["ln_in"] = n["own_in"] = n["lo_in"] = len(out)
 
+    done(Y.dma_start(T.fbd[:], T.fb[:]), "ld_fd", 16)
     done(Y.dma_start(T.at[:], T.an[:]), "ld_a", 16)
-    done(A.dma_start(T.fbd[:], T.fb[:]), "ld_fd", 16)
     for h in (0, 1):
         done(Y.dma_start(T.kt[:, 1024 * h:1024 * h + 1024], T.k[:, 1024 * h:1024 * h + 1024]), "ld_k%d" % h, 16)
     constants()
@@ -225,97 +231,112 @@ def rank_program(g, core, T, topo):
     done(V.quantize_mx(qa, qas, T.at[:]), "qa_ok")
 
     need(g, "ld_fd")
-    send("sf", (t["scales"], r1, "rf_in", T.fbd[:], T.rfb[:]), (t["codes"], r2, "rf_in", T.fbd[:], T.rfb[:]),
-         (t["helper"], out, "rf_in", T.fbd[:], T.rfb[:]))
+    send("sf", (t["scales"], out[0:4], "rf_in", T.fbd[:], T.rfb[:]), (t["codes2"], out[4:6], "rf_in", T.fbd[:], T.rfb[:]),
+         (dh, out[6:8], "rd_in", T.fbd[:], T.rfb[:]))
     need(g, "qa_ok")
-    send("sx", (t["codes"], chip, "ra_in", u8(qa), u8(T.rac[:])))
-    send("sx", (t["scales"], chip, "ra_in", qas, T.ras[:]))
+    send("sx", (t["codes"], out, "ra_in", u8(qa), u8(T.rac[:])))
+    send("sx", (t["scales"], rest, "ra_in", qas, T.ras[:]))
     send("sx", (dh, out, "a_in%d" % D_, u8(qa), u8(T.la[:, 0:128])))
-    send("sx", (dh, out, "a_in%d" % D_, qas, T.las[:, 0:128]))
-    for h, e in ((0, rest), (1, chip)):
+    for h in (0, 1):
         k = slice(128 + 256 * h, 384 + 256 * h)
         need(V, "ld_k%d" % h)
-        done(V.quantize_mx(T.qx[:, k], T.qxs[:, k], T.kt[:, 1024 * h:1024 * h + 1024]), "qk_ok%d" % h)
-        need(g, "qk_ok%d" % h)
-        send("sk", (t["helper"], e, "hx_in%d" % h, u8(T.qx[:, k]), u8(T.hx[:, k])))
-        send("sk", (t["helper"], e, "hx_in%d" % h, T.qxs[:, k], T.hxs[:, k]))
+        done(V.quantize_mx(T.qx[:, k], T.qxs[:, k], T.kt[:, 1024 * h:1024 * h + 1024]), "qk_ok")
+    need(g, "qk_ok")
+    send("sk", (t["helper"], rest, "hx_in", T.qxs[:, 128:640], T.hxs[:, 128:640]))
+    send("sx", (dh, out, "a_in%d" % D_, qas, T.las[:, 0:128]))
+    send("sk", (t["helper"], chip, "hx_in", u8(T.qx[:, 128:640]), u8(T.hx[:, 128:640])))
 
-    need(Y, "sx", "qk_ok1")
+    need(Y, "sx")
     done(Y.dma_start(T.vt[:], T.v[:]), "ld_v", 16)
     done(Y.dma_start(T.ut[:], T.u[:]), "ld_u", 16)
 
-    pieces = ([(0, 128, T.p0, ["qk_ok0", "a_in0"]), (128, 256, T.p1, []), (256, 512, T.p2, ["qk_ok1"])],
-              [(0, 256, T.p3, ["a_in1"]), (256, 512, T.p4, [])])
-    need(V, "f_in%d" % A_, "f_in%d" % B_)
-    penalties(512 * rank)
-    for i in (A_, B_):
-        search(i, T.la[:, col[i]], T.las[:, col[i]], T.qx, T.qxs, pieces[i])
-        masked(i, T["run%d" % i][:, 512:513])
-        need(g, "idx_ok%d" % i)
-        send("sent", (t[("codes2", "scales")[i]], chip, "rb_in", T["run%d" % i][:, 511:513], T.rbest[:]))
-
-    lists = ((T.off[:, 0:8], "off_ok0"), (T.off[:, 8:16], "off_ok1"), (T.lo[:], "lo_in"))
-    for step in STEPS.split():
-        i = "ABD".index(step[1])
-        if step[0] in "TGR":
-            turn(i, step[0])
-            continue
-        if step[0] in "vs":
-            k = int(step[2])
-            to, frm = T["z%d" % i][:, k:512:4], T.vt[:, k:2048].indirect(lists[i][0])
-            need(V if step[0] == "v" else A, "ld_v", lists[i][1])
-            done(V.tensor_copy(to, frm) if step[0] == "v" else A.activation(to, frm, ACT.Copy), "z%s_ok%d" % (step[0], i))
-            continue
-        zq, zqs = T["zq%d" % i][:], T["zqs%d" % i][:]
-        need(V, "zv_ok%d" % i, "zs_ok%d" % i)
-        done(V.quantize_mx(zq, zqs, T["z%d" % i][:]), "zq_ok%d" % i)
-        need(g, "zq_ok%d" % i)
-        if i == D_:
-            send("sent", (dm, out, "z_in%d" % D_, u8(zq), u8(T.lz[:, col[D_]])))
-            send("sent", (dm, out, "z_in%d" % D_, zqs, T.lzs[:, col[D_]]))
-        else:
-            send("sent", (t[("codes", "codes2")[i]], chip, "rz_in", u8(zq), u8(T.rzc[:])))
-            send("sent", (t["scales"], chip, "rs_in%d" % i, zqs, T.rzs[:, col[i]]))
-
     place = [128 * q + (384 if q > rank else 0) for q in range(N)]
     own = N - 1 - rank
-    need(V, "ld_u", "pos_in", "ln_in")
+    need(V, "pos_in", "ln_in")
     done(V.tensor_scalar(T.pos[:], T.ln[:], 0.25, T.lp[:], OP.mult, OP.add), "m0")
-    done(V.quantize_mx(T.qu[:], T.qus[:], T.ut[:]), "qu_ok")
     need(V, "m0")
     if own > 0:
-        done(V.tensor_scalar(T.pos[:, 0:own], T.pos[:, 0:own], 384.0, None, OP.add), "m2")
-    done(V.quantize_mx(T.qv[:], T.qvs[:], T.vt[:]), "qv_ok")
-    need(V, "own_in", "b_in0", "b_in1", "b_in2")
-    done(V.tensor_reduce(T.mx[:], T.best[:, 0:16:4], AxisListType.X, OP.max), "m1")
-    done(V.tensor_scalar(T.pos[:, own:own + 1], T.best[:, 4 * own + 1:4 * own + 2], float(place[rank]), None, OP.add), "m2")
-    done(V.tensor_tensor(T.gl[:], T.best[:, 1:16:4], T.ln[:], OP.add), "m2")
-    need(V, "m1")
-    done(V.tensor_scalar(T.lt[:], T.best[:, 0:16:4], T.mx[:], None, OP.is_lt), "m3")
-    need(V, "m2", "m3")
-    done(V.tensor_tensor_scan(T.pick[:], T.lt[:], T.pos[:], 0.0, OP.mult, OP.max), "pick_ok")
-    done(V.tensor_tensor_scan(T.won[:], T.lt[:], T.gl[:], 0.0, OP.mult, OP.max), "won_ok")
-    need(Y, "won_ok")
-    done(Y.dma_start(T.win[:], T.won[:, 3:4]), "st", 16)
-    need(V, "pick_ok")
-    done(V.tensor_scalar(T.x[:, 128:192], T.mask[:], T.pick[:, 3:4], 0.25, OP.mult, OP.mult), "x_ok2")
-    turn(2)
+        done(V.tensor_scalar(T.pos[:, 0:own], T.pos[:, 0:own], 384.0, None, OP.add), "m0")
+    need(V, "f_in%d" % A_, "f_in%d" % B_)
+    penalties(512 * rank, A_, B_)
 
-    need(P, "qu_ok", "qv_ok")
-    done(P.matmul_mx(T.p4[:], T.qu[:], T.qus[:], T.qv[:], T.qvs[:], True, True), "pu_ok3")
-    need(A, "pu_ok3")
-    done(A.activation(T.prod[:, place[rank]:place[rank] + 512], T.p4[:], ACT.Copy), "us")
+    pieces = ([(0, 128, T.p0, ["qk_ok", "a_in0"]), (128, 256, T.p1, []), (256, 512, T.p2, [])],
+              [(0, 256, T.p3, ["a_in1"]), (256, 512, T.p4, [])])
+    lists = ((T.off[:, 0:8], "off_ok0"), (T.off[:, 8:16], "off_ok1"), (T.lo[:], "lo_in"))
+
+    def product(bank, codes, scales, at, ready, by):
+        frm, to = T["p%d" % bank][:, 0:128], T.prod[:, at:at + 128]
+        need(P, "qu_ok", ready)
+        done(P.matmul_mx(frm, T.qu[:], T.qus[:], codes, scales, True, True), "pu_ok%d" % bank)
+        need(by, "pu_ok%d" % bank)
+        done(V.tensor_copy(to, frm) if by is V else A.activation(to, frm, ACT.Copy), "uv" if by is V else "us")
+
+    for step in STEPS.split():
+        do, i = step[0], "ABD".find(step[1])
+        if do == "m":
+            h = int(step[2])
+            scores(i, h, T.la[:, col[i]], T.las[:, col[i]], T.qx, T.qxs, *pieces[i][h])
+        elif do in "lhw":
+            last = len(pieces[i]) - 1
+            running(i, *{"l": (0, 256, range(last)), "h": (256, 512, [last]), "w": (0, 512, range(last + 1))}[do])
+            if do != "l":
+                masked(i)
+                need(g, "idx_ok%d" % i)
+                send("sent", (t[("codes", "scales")[i]], chip, "rb_in", T["run%d" % i][:, 511:513], T.rbest[:]))
+        elif do in "TGR":
+            turn(*((2, do, 4) if step[1] == "P" else (i, do)))
+        elif do in "vs":
+            k = int(step[2])
+            to, frm = T["z%d" % i][:, k:512:4], T.vt[:, k:2048].indirect(lists[i][0])
+            need(V if do == "v" else A, "ld_v", lists[i][1])
+            done(V.tensor_copy(to, frm) if do == "v" else A.activation(to, frm, ACT.Copy), "z%s_ok%d" % (do, i))
+        elif do == "Q":
+            zq, zqs = T["zq%d" % i][:], T["zq%ds" % i][:]
+            need(V, "zv_ok%d" % i, "zs_ok%d" % i)
+            done(V.quantize_mx(zq, zqs, T["z%d" % i][:]), "zq_ok%d" % i)
+            need(g, "zq_ok%d" % i)
+            if i == D_:
+                send("sent", (dm, out, "z_in%d" % D_, u8(zq), u8(T.lz[:, col[D_]])))
+                send("sent", (dm, out, "z_in%d" % D_, zqs, T.lzs[:, col[D_]]))
+            else:
+                for call in BACK[i]:
+                    e = len(chip) // len(call)
+                    send("sent", *[(t[job], chip[e * j:e * j + e], "r%s_in%d" % (kind, i), piece(T, "zq%d" % i, kind, c0, c1),
+                                    piece(T, "rz", kind, 128 * i + c0, 128 * i + c1)) for j, (kind, c0, c1, job) in enumerate(call)])
+        elif do == "p":
+            k = int(step[2])
+            c = slice(128 * k, 128 * k + 128)
+            need(V, "ld_v")
+            done(V.quantize_mx(T.qv[:, c], T.qvs[:, c], T.vt[:, 512 * k:512 * k + 512]), "qv_ok%d" % k)
+            product(k, T.qv[:, c], T.qvs[:, c], place[rank] + 128 * k, "qv_ok%d" % k, A)
+        elif step == "cU":
+            need(V, "ld_u")
+            done(V.quantize_mx(T.qu[:], T.qus[:], T.ut[:]), "qu_ok")
+        elif step == "cX":
+            need(V, "own_in", "b_in0", "b_in1", "b_in2")
+            done(V.tensor_reduce(T.mx[:], T.best[:, 0:16:4], AxisListType.X, OP.max), "m1")
+        elif step == "cN":
+            need(V, "m0")
+            done(V.tensor_scalar(T.pos[:, own:own + 1], T.best[:, 4 * own + 1:4 * own + 2], float(place[rank]), None, OP.add), "m2")
+        elif step == "cW":
+            done(V.tensor_tensor(T.gl[:], T.best[:, 1:16:4], T.ln[:], OP.add), "m4")
+        elif step == "cL":
+            need(V, "m1")
+            done(V.tensor_scalar(T.lt[:], T.best[:, 0:16:4], T.mx[:], None, OP.is_lt), "m3")
+        elif step == "cP":
+            need(V, "m2", "m3")
+            done(V.tensor_tensor_scan(T.pick[:], T.lt[:], T.pos[:], 0.0, OP.mult, OP.max), "pick_ok")
+        elif step == "cK":
+            need(V, "pick_ok")
+            done(V.tensor_scalar(T.x[:, 128:160], T.mask[:], T.pick[:, 3:4], 0.25, OP.mult, OP.mult), "x_ok2")
+        elif step == "cG":
+            need(V, "m3", "m4")
+            done(V.tensor_tensor_scan(T.won[:], T.lt[:], T.gl[:], 0.0, OP.mult, OP.max), "won_ok")
+            need(Y, "won_ok")
+            done(Y.dma_start(T.win[:], T.won[:, 3:4]), "st", 16)
+
     for i in (A_, D_, B_):
-        frm = T["p%d" % (5 + i)][:, 0:128]
-        to = T.prod[:, place[t["ranks"][i]]:place[t["ranks"][i]] + 128]
-        need(P, "z_in%d" % i)
-        done(P.matmul_mx(frm, T.qu[:], T.qus[:], T.lz[:, col[i]], T.lzs[:, col[i]], True, True), "pu_ok%d" % i)
-        if i == B_:
-            need(V, "pu_ok%d" % i)
-            done(V.tensor_copy(to, frm), "uv")
-        else:
-            need(A, "pu_ok%d" % i)
-            done(A.activation(to, frm, ACT.Copy), "us")
+        product(5 + i, T.lz[:, col[i]], T.lzs[:, col[i]], place[t["ranks"][i]], "z_in%d" % i, V if i == B_ else A)
     need(V, "off_ok2", "uv", "us")
     need(A, "off_ok2", "uv", "us")
     done(V.tensor_copy(T.ysb[:, 0:64], T.prod[:].indirect(T.off[:, 16:20])), "yv_ok")
@@ -328,30 +349,32 @@ def rank_program(g, core, T, topo):
 
 def helper_program(g, core, T, topo, r, t, job):
     V, Y = g.vector, g.sync
-    n, done, need, send, constants, penalties, search, masked, turn = tools(g, core, T, topo)
+    n, done, need, send, constants, penalties, scores, running, masked, turn = tools(g, core, T, topo)
     me, dm = T.cores[r], T.cores[t["ranks"][D_]]
-    chip, out = topo.engines(core, me), topo.engines(core, dm)
-    n["rf_in"] = n["rd_in"] = len(out)
-    n["a_in%d" % D_] = n["hx_in0"] = n["ra_in"] = 2 * len(out)
-    n["hx_in1"] = 2 * len(chip)
-    need(Y, "rf_in")
-    done(Y.dma_start(T.lf[:, 1:2], T.rfb[:]), "ld_f", 16)
+    out = topo.engines(core, dm)
+    n["rf_in"], n["rd_in"] = len(out), len(out) // 4
+    n["a_in%d" % D_] = n["ra_in"] = 2 * len(out)
+    n["hx_in"] = 3 * len(out)
+    need(Y, "rd_in")
+    done(Y.dma_start(T.lf[:, 0:1], T.rfb[:]), "ld_f", 16)
     constants()
-    need(g, "rf_in")
-    send("sent", (team(T, topo, t["ranks"][D_])["helper"], out, "rd_in", T.rfb[:], T.lf[:, 0:1]))
-    need(V, "ld_f", "rd_in")
-    penalties(512 * r)
+    need(V, "ld_f")
+    penalties(512 * r, 0)
     own = len(T.cores) - 1 - r
     slot = T.best[:, 4 * own:4 * own + 2]
-    search(0, T.la[:, 0:128], T.las[:, 0:128], T.hx, T.hxs,
-           [(0, 256, T.p0, ["hx_in0", "a_in%d" % D_]), (256, 512, T.p1, ["hx_in1"])], True)
-    masked(0, T.run0[:, 512:513])
+    for h, ready in enumerate((["hx_in", "a_in%d" % D_], [])):
+        scores(0, h, T.la[:, 0:128], T.las[:, 0:128], T.hx, T.hxs, 256 * h, 256 * h + 256, T["p%d" % h], ready)
+    running(0, 0, 512, [0, 1])
+    masked(0)
+    need(V, "rf_in")
+    penalties(512 * r, 1)
+    scores(1, 0, T.hx[:, 0:128], T.hxs[:, 0:128], T.hx, T.hxs, 0, 512, T.p2, ["ra_in"])
     need(g, "idx_ok0")
     send("sent", (dm, out, "b_in%d" % D_, T.run0[:, 511:513], slot))
     turn(0)
     need(g, "off_ok0")
     send("sent", (me, out, "lo_in", T.off[:, 0:8], T.lo[:]))
-    search(1, T.hx[:, 0:128], T.hxs[:, 0:128], T.hx, T.hxs, [(0, 512, T.p2, ["ra_in"])])
+    running(1, 0, 512, [0])
     need(g, "idx_ok1")
     send("sent", (me, out, "own_in", T.run1[:, 511:513], slot))
     need(g, "sent")
@@ -367,14 +390,13 @@ def relay_program(g, core, T, topo, r, t, job):
     chip = topo.engines(me, core)
     rest = [e for e in chip if e not in out]
     col = [slice(128 * i, 128 * i + 128) for i in range(2)]
-    n["rf_in"] = len(chip) // 4
-    n["ra_in"] = n["rb_in"] = n["rz_in"] = n["rs_in0"] = n["rs_in1"] = len(chip)
+    n["rf_in"], n["ra_in"] = len(out) // (2 if job == "scales" else 4), len(out)
+    n["rb_in"] = len(chip)
     if job == "codes":
-        done(g.iota(T.cp[:], [[0, 1]], 0, 1, allow_small_or_imprecise_dtypes=True), "k0")
+        for a, first in enumerate((0, 64, 32, 96)):
+            done(g.iota(T.cp[32 * a:32 * a + 32, :], [[0, 1]], first, 1, allow_small_or_imprecise_dtypes=True), "k0")
         need(g, "k0")
         send("sent", (to[A_], out, "pos_in", T.cp[:], T.lp[:]))
-        need(g, "rf_in")
-        send("sent", (to[B_], out, "f_in%d" % B_, T.rfb[:], T.lf[:, B_:B_ + 1]))
         need(g, "ra_in")
         for i in (A_, B_):
             send("sent", (to[i], out, "a_in%d" % i, u8(T.rac[:]), u8(T.la[:, col[i]])))
@@ -385,21 +407,24 @@ def relay_program(g, core, T, topo, r, t, job):
         need(g, "k1")
         send("sent", (to[A_], out, "ln_in", T.cn[:], T.ln[:]))
         need(g, "rf_in")
-        send("sent", (to[A_], out, "f_in%d" % A_, T.rfb[:], T.lf[:, A_:A_ + 1]))
+        send("sent", *[(to[i], out[4 * i:4 * i + 4], "f_in%d" % i, T.rfb[:], T.lf[:, i:i + 1]) for i in (A_, B_)])
         need(g, "ra_in")
         for i in (A_, B_):
             send("sent", (to[i], out, "a_in%d" % i, T.ras[:], T.las[:, col[i]]))
         send("sent", (t["helper"], rest, "ra_in", T.ras[:], T.hxs[:, 0:128]))
-    if job != "codes":
-        i = A_ if job == "codes2" else B_
-        need(g, "rb_in")
-        send("sent", (to[i], out, "b_in%d" % i, T.rbest[:], T.best[:, 4 * (N - 1 - r):4 * (N - 1 - r) + 2]))
-    if job == "scales":
-        for i in (A_, B_):
-            need(g, "rs_in%d" % i)
-            send("sent", (to[i], out, "z_in%d" % i, T.rzs[:, col[i]], T.lzs[:, col[i]]))
+    if job == "codes2":
+        need(g, "rf_in")
+        send("sent", (t["helper"], out, "rf_in", T.rfb[:], T.lf[:, 1:2]))
     else:
         i = A_ if job == "codes" else B_
-        need(g, "rz_in")
-        send("sent", (to[i], out, "z_in%d" % i, u8(T.rzc[:]), u8(T.lz[:, col[i]])))
+        need(g, "rb_in")
+        send("sent", (to[i], out, "b_in%d" % i, T.rbest[:], T.best[:, 4 * (N - 1 - r):4 * (N - 1 - r) + 2]))
+    for i in (A_, B_):
+        for call in BACK[i]:
+            for kind, c0, c1, by in call:
+                if by == job:
+                    n["r%s_in%d" % (kind, i)] = len(chip) // len(call)
+                    need(g, "r%s_in%d" % (kind, i))
+                    c0, c1 = 128 * i + c0, 128 * i + c1
+                    send("sent", (to[i], out, "z_in%d" % i, piece(T, "rz", kind, c0, c1), piece(T, "lz", kind, c0, c1)))
     need(g, "sent")

from concourse.bass import DstId, RemoteDMATransfer
from concourse.mybir import dt, AluOpType, AxisListType, ActivationFunctionType

OP = AluOpType
ACT = ActivationFunctionType
C8 = "float8_e4m3fn_x4"
FAR = 1.0e29
A_, B_, D_ = 0, 1, 2
JOBS = ("codes", "scales", "codes2", "helper")
STEPS = ("mA0 mA1 mA2 wA mB0 mB1 wB TA GA RA sA0 sA1 sA2 vA3 TB GB RB QA sB2 sB3 vB0 vB1 QB sD1 sD2 sD3 cU vD0 pV0 pV1 cX QD "
         "cN cL pV2 cP pV3 cK cW TP cG GP RP")
BACK = ([[("c", 0, 128, "codes")], [("s", 0, 128, "scales")]],
        [[("c", 0, 64, "codes2"), ("c", 64, 128, "scales")], [("s", 0, 128, "codes")]])

SCRATCH = {
    "at": ("sbuf", [128, 512], "bfloat16"),
    "kt": ("sbuf", [128, 2048], "bfloat16"),
    "vt": ("sbuf", [128, 2048], "bfloat16"),
    "ut": ("sbuf", [128, 512], "bfloat16"),
    "fbd": ("dram", [128, 1], "int32"),
    "qx": ("sbuf", [128, 640], C8), "qxs": ("sbuf", [128, 640], "uint8"),
    "qu": ("sbuf", [128, 128], C8), "qus": ("sbuf", [128, 128], "uint8"),
    "qv": ("sbuf", [128, 512], C8), "qvs": ("sbuf", [128, 512], "uint8"),
    "la": ("sbuf", [128, 256], C8), "las": ("sbuf", [128, 256], "uint8"),
    "lf": ("sbuf", [128, 4], "int32"),
    "best": ("sbuf", [128, 16], "float32"),
    "lz": ("sbuf", [128, 384], C8), "lzs": ("sbuf", [128, 384], "uint8"),
    "lp": ("sbuf", [128, 1], "float32"), "ln": ("sbuf", [128, 4], "bfloat16"),
    "lo": ("sbuf", [128, 8], "uint16"),
    "rfb": ("dram", [128, 1], "int32"),
    "rac": ("sbuf", [128, 128], C8), "ras": ("sbuf", [128, 128], "uint8"),
    "rbest": ("sbuf", [128, 2], "float32"),
    "rz": ("sbuf", [128, 256], C8), "rzs": ("sbuf", [128, 256], "uint8"),
    "hx": ("sbuf", [128, 640], C8), "hxs": ("sbuf", [128, 640], "uint8"),
    "ones": ("sbuf", [128, 256], "bfloat16"),
    "num": ("sbuf", [128, 256], "bfloat16"),
    "im": ("sbuf", [128, 32], "int32"), "am": ("sbuf", [128, 32], "int32"),
    "mask": ("sbuf", [128, 32], "float32"),
    "keep": ("sbuf", [128, 64], "float32"),
    "cp": ("sbuf", [128, 1], "float32"), "cn": ("sbuf", [128, 4], "bfloat16"),
    "fn": ("sbuf", [128, 8], "float32"),
    "ab": ("sbuf", [128, 512], "bfloat16"),
    "x": ("sbuf", [128, 192], "float32"), "xt": ("sbuf", [128, 192], "float32"),
    "xw": ("sbuf", [128, 384], "float32"), "off": ("sbuf", [128, 24], "uint16"),
    "pos": ("sbuf", [128, 4], "float32"),
    "mx": ("sbuf", [128, 1], "float32"), "lt": ("sbuf", [128, 4], "float32"), "gl": ("sbuf", [128, 4], "float32"),
    "pick": ("sbuf", [128, 4], "float32"), "won": ("sbuf", [128, 4], "float32"),
    "prod": ("sbuf", [128, 896], "float32"),
    "ysb": ("sbuf", [128, 128], "float32"),
}
for _i in range(8):
    SCRATCH["p%d" % _i] = ("psum", [128, 512], "float32")
for _i in range(2):
    SCRATCH["pen%d" % _i] = ("sbuf", [128, 512], "bfloat16")
    SCRATCH["ms%d" % _i] = ("sbuf", [128, 512], "float32")
    SCRATCH["run%d" % _i] = ("sbuf", [128, 520], "float32")
    SCRATCH["sink%d" % _i] = ("sbuf", [128, 512], "bfloat16")
for _i in range(3):
    SCRATCH["z%d" % _i] = ("sbuf", [128, 512], "bfloat16")
    SCRATCH["zq%d" % _i] = ("sbuf", [128, 128], C8)
    SCRATCH["zq%ds" % _i] = ("sbuf", [128, 128], "uint8")

SEMAPHORES = (
    ["ld_a", "ld_k0", "ld_k1", "ld_v", "ld_u", "ld_fd", "ld_f", "st"]
    + ["sf", "sx", "sk", "sent"]
    + ["rf_in", "rd_in", "ra_in", "rb_in", "rc_in0", "rc_in1", "rs_in0", "rs_in1", "hx_in", "pos_in", "ln_in", "own_in", "lo_in"]
    + ["%s%d" % (n, i) for n in ("a_in", "f_in", "b_in", "z_in") for i in range(3)]
    + ["k0", "k1", "k2", "k3", "k4", "qa_ok", "qk_ok", "qu_ok", "ab_ok", "fn_ok"]
    + ["%s%d" % (n, i) for n in ("pen_ok", "mm0_ok", "mm1_ok", "mm2_ok", "ms0_ok", "ms1_ok", "ms2_ok", "run_ok", "idx_ok") for i in range(2)]
    + ["%s%d" % (n, i) for n in ("zv_ok", "zs_ok", "zq_ok", "x_ok", "xt_ok", "xw_ok", "off_ok") for i in range(3)]
    + ["pu_ok%d" % i for i in range(8)] + ["qv_ok%d" % i for i in range(4)]
    + ["m0", "m1", "m2", "m3", "m4", "pick_ok", "won_ok", "uv", "us", "yv_ok", "ys_ok"]
)


def bits(engines):
    m = 0
    for e in engines:
        m |= 1 << e
    return m


def u8(view):
    return view.bitcast(dt.uint8)


def piece(T, name, kind, c0, c1):
    return u8(T[name][:, c0:c1]) if kind == "c" else T[name + "s"][:, c0:c1]


def team(T, topo, r):
    me = T.cores[r]
    others = [q for q in range(len(T.cores)) if q != r]
    cross = sorted([q for q in others if not topo.may_write(me, T.cores[q])], key=lambda q: topo.host(T.cores[q]) != topo.host(me))
    direct = [q for q in others if q not in cross]
    free = [c for c in topo.cores_of(me) if c != me]
    ports = [c for c in free if topo.may_write(c, T.cores[cross[0]])]
    near = [c for c in ports if topo.die(c) == topo.die(me)]
    far = [c for c in ports if c not in near]
    helper = [c for c in free if c not in ports and topo.die(c) == topo.die(me)][0]
    return {"ranks": cross + direct, "codes": far[0], "scales": near[0], "codes2": far[1], "helper": helper}


def tools(g, core, T, topo):
    S = T.sem
    V, P, A = g.vector, g.tensor, g.scalar
    n = {}

    def done(q, name, k=1):
        q.then_inc(S[name], k)
        n[name] = n.get(name, 0) + k

    def need(queue, *names):
        for x in names:
            queue.wait_ge(S[x], n[x])

    def send(left, *moves):
        ts = []
        for dst, engines, sem, src, to in moves:
            rid, pid = topo.addr(dst, core)
            ts.append(RemoteDMATransfer(dst_ids=[DstId(rid=rid, pnc=pid)], dma_engine_mask=bits(engines), remote_sem=S[sem], src=src, dst=to))
            n[left] = n.get(left, 0) + len(engines)
        g.remote_dma_fused(ts, local_sem=S[left])

    def constants():
        done(g.iota(T.im[:], [[0, 2], [-1, 16]], 16, 1), "k0")
        done(V.memset(T.keep[:], 1.0), "k1")
        done(V.memset(T.ones[:], 1.0), "k1")
        need(V, "k1")
        done(V.tensor_tensor_scan(T.num[:], T.ones[:], T.ones[:], -1.0, OP.add, OP.mult), "k2")
        done(V.memset(T.keep[:, 0:64:16], 0.0), "k2")
        need(V, "k0")
        done(V.tensor_scalar(T.am[:], T.im[:], 15, None, OP.bitwise_and), "k3")
        need(V, "k3")
        done(V.tensor_scalar(T.mask[:], T.am[:], 0.0, 4.0, OP.is_equal, OP.mult), "k4")
        need(V, "k2", "k4")
        need(A, "k2", "k4")

    def penalties(first, i, j=None):
        e = i + 1 if j is None else j + 1
        half = [slice(256 * h, 256 * h + 256) for h in (0, 1)]
        for h in (0, 1):
            done(V.tensor_scalar(T.fn[:, 4 * h + i:4 * h + e], T.lf[:, i:e], float(first + 256 * h), None, OP.subtract), "fn_ok")
        need(V, "fn_ok")
        for h in (0, 1):
            done(V.tensor_scalar(T["pen%d" % i][:, half[h]], T.num[:], T.fn[:, 4 * h + i:4 * h + i + 1], FAR, OP.is_equal, OP.mult), "pen_ok%d" % i)
        if j is not None:
            need(A, "fn_ok")
            for h in (0, 1):
                done(A.activation(T.ab[:, half[h]], T.num[:], ACT.Abs, bias=T.fn[:, 4 * h + j:4 * h + j + 1], scale=-1.0), "ab_ok")
            need(A, "ab_ok")
            done(A.activation(T["pen%d" % j][:], T.ab[:], ACT.Relu, bias=FAR, scale=-FAR), "pen_ok%d" % j)

    def scores(i, h, anchors, scales, q, qs, c0, c1, bank, ready):
        c, k = slice(c0, c1), slice(128 + c0, 128 + c1)
        need(P, *ready)
        done(P.matmul_mx(bank[:, 0:c1 - c0], anchors, scales, q[:, k], qs[:, k], True, True), "mm%d_ok%d" % (h, i))
        need(V, "pen_ok%d" % i, "mm%d_ok%d" % (h, i))
        done(V.tensor_tensor(T["ms%d" % i][:, c], bank[:, 0:c1 - c0], T["pen%d" % i][:, c], OP.subtract), "ms%d_ok%d" % (h, i))

    def running(i, c0, c1, pieces):
        m, r = T["ms%d" % i], T["run%d" % i]
        need(V, *["ms%d_ok%d" % (h, i) for h in pieces])
        if c0:
            need(V, "run_ok%d" % i)
        done(V.tensor_tensor_scan(r[:, c0:c1], m[:, c0:c1], m[:, c0:c1], r[:, c0 - 1:c0] if c0 else -FAR, OP.max, OP.max), "run_ok%d" % i)
        if c1 == 512:
            need(A, "run_ok%d" % i)
            done(A.activation(T["sink%d" % i][:], r[:, 0:512], ACT.Sign, bias=r[:, 511:512], scale=-1.0, accum_out=r[:, 512:513]), "idx_ok%d" % i)

    def masked(l):
        need(A, "idx_ok%d" % l)
        for h in (0, 1):
            p, c = slice(64 * h, 64 * h + 64), slice(64 * l + 32 * h, 64 * l + 32 * h + 32)
            done(A.activation(T.x[0:64, c], T.mask[p, :], ACT.Identity, scale=T["run%d" % l][p, 512:513]), "x_ok%d" % l)

    def turn(l, steps="TGR", blocks=2):
        w = 128 // blocks
        c = slice(64 * l, 64 * l + w)
        if "T" in steps:
            need(V, "x_ok%d" % l)
            done(V.transpose(T.xt[0:32 * blocks, c], T.x[0:32 * blocks, c]), "xt_ok%d" % l)
        if "G" in steps:
            need(V, "xt_ok%d" % l)
            for a in range(blocks):
                b = slice(32 * a, 32 * a + 32)
                done(V.tensor_tensor_scan(T.xw[0:32, 128 * l + w * a:128 * l + w * a + w], T.keep[b, 0:w], T.xt[b, c], 0.0, OP.mult, OP.add),
                     "xw_ok%d" % l)
        if "R" in steps:
            need(V, "xw_ok%d" % l)
            for a in range(4):
                done(V.tensor_copy(T.off[32 * a:32 * a + 32, 8 * l:8 * l + 8], T.xw[0:32, 128 * l + 15:128 * l + 128:16]), "off_ok%d" % l)

    return n, done, need, send, constants, penalties, scores, running, masked, turn


def rank_program(g, core, T, topo):
    rank = T.rank_of(core)
    if rank is None:
        for r in range(len(T.cores)):
            t = team(T, topo, r)
            for job in JOBS:
                if t[job] == core:
                    (helper_program if job == "helper" else relay_program)(g, core, T, topo, r, t, job)
        return
    N = len(T.cores)
    t = team(T, topo, rank)
    V, P, A, Y = g.vector, g.tensor, g.scalar, g.sync
    n, done, need, send, constants, penalties, scores, running, masked, turn = tools(g, core, T, topo)
    dm = T.cores[t["ranks"][D_]]
    dh = team(T, topo, t["ranks"][D_])["helper"]
    out = topo.engines(core, dm)
    chip = topo.engines(core, t["helper"])
    rest = [e for e in chip if e not in out]
    col = [slice(128 * i, 128 * i + 128) for i in range(3)]
    qa, qas = T.qx[:, 0:128], T.qxs[:, 0:128]

    for i in range(3):
        n["a_in%d" % i] = n["z_in%d" % i] = 2 * len(out)
        n["b_in%d" % i], n["f_in%d" % i] = len(out), len(out) // 2
    for i in (A_, B_):
        n["z_in%d" % i] = len(out) * sum(len(call) for call in BACK[i])
    n["pos_in"] = n["ln_in"] = n["own_in"] = n["lo_in"] = len(out)

    done(Y.dma_start(T.fbd[:], T.fb[:]), "ld_fd", 16)
    done(Y.dma_start(T.at[:], T.an[:]), "ld_a", 16)
    for h in (0, 1):
        done(Y.dma_start(T.kt[:, 1024 * h:1024 * h + 1024], T.k[:, 1024 * h:1024 * h + 1024]), "ld_k%d" % h, 16)
    constants()
    need(V, "ld_a")
    done(V.quantize_mx(qa, qas, T.at[:]), "qa_ok")

    need(g, "ld_fd")
    send("sf", (t["scales"], out[0:4], "rf_in", T.fbd[:], T.rfb[:]), (t["codes2"], out[4:6], "rf_in", T.fbd[:], T.rfb[:]),
         (dh, out[6:8], "rd_in", T.fbd[:], T.rfb[:]))
    need(g, "qa_ok")
    send("sx", (t["codes"], out, "ra_in", u8(qa), u8(T.rac[:])))
    send("sx", (t["scales"], rest, "ra_in", qas, T.ras[:]))
    send("sx", (dh, out, "a_in%d" % D_, u8(qa), u8(T.la[:, 0:128])))
    for h in (0, 1):
        k = slice(128 + 256 * h, 384 + 256 * h)
        need(V, "ld_k%d" % h)
        done(V.quantize_mx(T.qx[:, k], T.qxs[:, k], T.kt[:, 1024 * h:1024 * h + 1024]), "qk_ok")
    need(g, "qk_ok")
    send("sk", (t["helper"], rest, "hx_in", T.qxs[:, 128:640], T.hxs[:, 128:640]))
    send("sx", (dh, out, "a_in%d" % D_, qas, T.las[:, 0:128]))
    send("sk", (t["helper"], chip, "hx_in", u8(T.qx[:, 128:640]), u8(T.hx[:, 128:640])))

    need(Y, "sx")
    done(Y.dma_start(T.vt[:], T.v[:]), "ld_v", 16)
    done(Y.dma_start(T.ut[:], T.u[:]), "ld_u", 16)

    place = [128 * q + (384 if q > rank else 0) for q in range(N)]
    own = N - 1 - rank
    need(V, "pos_in", "ln_in")
    done(V.tensor_scalar(T.pos[:], T.ln[:], 0.25, T.lp[:], OP.mult, OP.add), "m0")
    need(V, "m0")
    if own > 0:
        done(V.tensor_scalar(T.pos[:, 0:own], T.pos[:, 0:own], 384.0, None, OP.add), "m0")
    need(V, "f_in%d" % A_, "f_in%d" % B_)
    penalties(512 * rank, A_, B_)

    pieces = ([(0, 128, T.p0, ["qk_ok", "a_in0"]), (128, 256, T.p1, []), (256, 512, T.p2, [])],
              [(0, 256, T.p3, ["a_in1"]), (256, 512, T.p4, [])])
    lists = ((T.off[:, 0:8], "off_ok0"), (T.off[:, 8:16], "off_ok1"), (T.lo[:], "lo_in"))

    def product(bank, codes, scales, at, ready, by):
        frm, to = T["p%d" % bank][:, 0:128], T.prod[:, at:at + 128]
        need(P, "qu_ok", ready)
        done(P.matmul_mx(frm, T.qu[:], T.qus[:], codes, scales, True, True), "pu_ok%d" % bank)
        need(by, "pu_ok%d" % bank)
        done(V.tensor_copy(to, frm) if by is V else A.activation(to, frm, ACT.Copy), "uv" if by is V else "us")

    for step in STEPS.split():
        do, i = step[0], "ABD".find(step[1])
        if do == "m":
            h = int(step[2])
            scores(i, h, T.la[:, col[i]], T.las[:, col[i]], T.qx, T.qxs, *pieces[i][h])
        elif do in "lhw":
            last = len(pieces[i]) - 1
            running(i, *{"l": (0, 256, range(last)), "h": (256, 512, [last]), "w": (0, 512, range(last + 1))}[do])
            if do != "l":
                masked(i)
                need(g, "idx_ok%d" % i)
                send("sent", (t[("codes", "scales")[i]], chip, "rb_in", T["run%d" % i][:, 511:513], T.rbest[:]))
        elif do in "TGR":
            turn(*((2, do, 4) if step[1] == "P" else (i, do)))
        elif do in "vs":
            k = int(step[2])
            to, frm = T["z%d" % i][:, k:512:4], T.vt[:, k:2048].indirect(lists[i][0])
            need(V if do == "v" else A, "ld_v", lists[i][1])
            done(V.tensor_copy(to, frm) if do == "v" else A.activation(to, frm, ACT.Copy), "z%s_ok%d" % (do, i))
        elif do == "Q":
            zq, zqs = T["zq%d" % i][:], T["zq%ds" % i][:]
            need(V, "zv_ok%d" % i, "zs_ok%d" % i)
            done(V.quantize_mx(zq, zqs, T["z%d" % i][:]), "zq_ok%d" % i)
            need(g, "zq_ok%d" % i)
            if i == D_:
                send("sent", (dm, out, "z_in%d" % D_, u8(zq), u8(T.lz[:, col[D_]])))
                send("sent", (dm, out, "z_in%d" % D_, zqs, T.lzs[:, col[D_]]))
            else:
                for call in BACK[i]:
                    e = len(chip) // len(call)
                    send("sent", *[(t[job], chip[e * j:e * j + e], "r%s_in%d" % (kind, i), piece(T, "zq%d" % i, kind, c0, c1),
                                    piece(T, "rz", kind, 128 * i + c0, 128 * i + c1)) for j, (kind, c0, c1, job) in enumerate(call)])
        elif do == "p":
            k = int(step[2])
            c = slice(128 * k, 128 * k + 128)
            need(V, "ld_v")
            done(V.quantize_mx(T.qv[:, c], T.qvs[:, c], T.vt[:, 512 * k:512 * k + 512]), "qv_ok%d" % k)
            product(k, T.qv[:, c], T.qvs[:, c], place[rank] + 128 * k, "qv_ok%d" % k, A)
        elif step == "cU":
            need(V, "ld_u")
            done(V.quantize_mx(T.qu[:], T.qus[:], T.ut[:]), "qu_ok")
        elif step == "cX":
            need(V, "own_in", "b_in0", "b_in1", "b_in2")
            done(V.tensor_reduce(T.mx[:], T.best[:, 0:16:4], AxisListType.X, OP.max), "m1")
        elif step == "cN":
            need(V, "m0")
            done(V.tensor_scalar(T.pos[:, own:own + 1], T.best[:, 4 * own + 1:4 * own + 2], float(place[rank]), None, OP.add), "m2")
        elif step == "cW":
            done(V.tensor_tensor(T.gl[:], T.best[:, 1:16:4], T.ln[:], OP.add), "m4")
        elif step == "cL":
            need(V, "m1")
            done(V.tensor_scalar(T.lt[:], T.best[:, 0:16:4], T.mx[:], None, OP.is_lt), "m3")
        elif step == "cP":
            need(V, "m2", "m3")
            done(V.tensor_tensor_scan(T.pick[:], T.lt[:], T.pos[:], 0.0, OP.mult, OP.max), "pick_ok")
        elif step == "cK":
            need(V, "pick_ok")
            done(V.tensor_scalar(T.x[:, 128:160], T.mask[:], T.pick[:, 3:4], 0.25, OP.mult, OP.mult), "x_ok2")
        elif step == "cG":
            need(V, "m3", "m4")
            done(V.tensor_tensor_scan(T.won[:], T.lt[:], T.gl[:], 0.0, OP.mult, OP.max), "won_ok")
            need(Y, "won_ok")
            done(Y.dma_start(T.win[:], T.won[:, 3:4]), "st", 16)

    for i in (A_, D_, B_):
        product(5 + i, T.lz[:, col[i]], T.lzs[:, col[i]], place[t["ranks"][i]], "z_in%d" % i, V if i == B_ else A)
    need(V, "off_ok2", "uv", "us")
    need(A, "off_ok2", "uv", "us")
    done(V.tensor_copy(T.ysb[:, 0:64], T.prod[:].indirect(T.off[:, 16:20])), "yv_ok")
    done(A.activation(T.ysb[:, 64:128], T.prod[:].indirect(T.off[:, 20:24]), ACT.Copy), "ys_ok")
    need(Y, "yv_ok", "ys_ok")
    done(Y.dma_start(T.y[:], T.ysb[:]), "st", 16)
    need(Y, "st")
    need(g, "sf", "sk", "sent")


def helper_program(g, core, T, topo, r, t, job):
    V, Y = g.vector, g.sync
    n, done, need, send, constants, penalties, scores, running, masked, turn = tools(g, core, T, topo)
    me, dm = T.cores[r], T.cores[t["ranks"][D_]]
    out = topo.engines(core, dm)
    n["rf_in"], n["rd_in"] = len(out), len(out) // 4
    n["a_in%d" % D_] = n["ra_in"] = 2 * len(out)
    n["hx_in"] = 3 * len(out)
    need(Y, "rd_in")
    done(Y.dma_start(T.lf[:, 0:1], T.rfb[:]), "ld_f", 16)
    constants()
    need(V, "ld_f")
    penalties(512 * r, 0)
    own = len(T.cores) - 1 - r
    slot = T.best[:, 4 * own:4 * own + 2]
    for h, ready in enumerate((["hx_in", "a_in%d" % D_], [])):
        scores(0, h, T.la[:, 0:128], T.las[:, 0:128], T.hx, T.hxs, 256 * h, 256 * h + 256, T["p%d" % h], ready)
    running(0, 0, 512, [0, 1])
    masked(0)
    need(V, "rf_in")
    penalties(512 * r, 1)
    scores(1, 0, T.hx[:, 0:128], T.hxs[:, 0:128], T.hx, T.hxs, 0, 512, T.p2, ["ra_in"])
    need(g, "idx_ok0")
    send("sent", (dm, out, "b_in%d" % D_, T.run0[:, 511:513], slot))
    turn(0)
    need(g, "off_ok0")
    send("sent", (me, out, "lo_in", T.off[:, 0:8], T.lo[:]))
    running(1, 0, 512, [0])
    need(g, "idx_ok1")
    send("sent", (me, out, "own_in", T.run1[:, 511:513], slot))
    need(g, "sent")


def relay_program(g, core, T, topo, r, t, job):
    V = g.vector
    n, done, need, send = tools(g, core, T, topo)[:4]
    N = len(T.cores)
    me = T.cores[r]
    to = [T.cores[q] for q in t["ranks"][:2]]
    out = topo.engines(core, to[0])
    chip = topo.engines(me, core)
    rest = [e for e in chip if e not in out]
    col = [slice(128 * i, 128 * i + 128) for i in range(2)]
    n["rf_in"], n["ra_in"] = len(out) // (2 if job == "scales" else 4), len(out)
    n["rb_in"] = len(chip)
    if job == "codes":
        for a, first in enumerate((0, 64, 32, 96)):
            done(g.iota(T.cp[32 * a:32 * a + 32, :], [[0, 1]], first, 1, allow_small_or_imprecise_dtypes=True), "k0")
        need(g, "k0")
        send("sent", (to[A_], out, "pos_in", T.cp[:], T.lp[:]))
        need(g, "ra_in")
        for i in (A_, B_):
            send("sent", (to[i], out, "a_in%d" % i, u8(T.rac[:]), u8(T.la[:, col[i]])))
        send("sent", (t["helper"], rest, "ra_in", u8(T.rac[:]), u8(T.hx[:, 0:128])))
    if job == "scales":
        for q in range(N):
            done(V.memset(T.cn[:, N - 1 - q:N - q], float(512 * q)), "k1")
        need(g, "k1")
        send("sent", (to[A_], out, "ln_in", T.cn[:], T.ln[:]))
        need(g, "rf_in")
        send("sent", *[(to[i], out[4 * i:4 * i + 4], "f_in%d" % i, T.rfb[:], T.lf[:, i:i + 1]) for i in (A_, B_)])
        need(g, "ra_in")
        for i in (A_, B_):
            send("sent", (to[i], out, "a_in%d" % i, T.ras[:], T.las[:, col[i]]))
        send("sent", (t["helper"], rest, "ra_in", T.ras[:], T.hxs[:, 0:128]))
    if job == "codes2":
        need(g, "rf_in")
        send("sent", (t["helper"], out, "rf_in", T.rfb[:], T.lf[:, 1:2]))
    else:
        i = A_ if job == "codes" else B_
        need(g, "rb_in")
        send("sent", (to[i], out, "b_in%d" % i, T.rbest[:], T.best[:, 4 * (N - 1 - r):4 * (N - 1 - r) + 2]))
    for i in (A_, B_):
        for call in BACK[i]:
            for kind, c0, c1, by in call:
                if by == job:
                    n["r%s_in%d" % (kind, i)] = len(chip) // len(call)
                    need(g, "r%s_in%d" % (kind, i))
                    c0, c1 = 128 * i + c0, 128 * i + c1
                    send("sent", (to[i], out, "z_in%d" % i, piece(T, "rz", kind, c0, c1), piece(T, "lz", kind, c0, c1)))
    need(g, "sent")
